import numpy as np, ml_dtypes
CORES = [40,41,42,43,44,45,46,47]
N = 8
BF = ml_dtypes.bfloat16
def gentries(a):
    return np.ascontiguousarray(a.reshape(8, 16, -1).transpose(0, 2, 1)).reshape(8, -1)
def gtable(e):
    e = np.asarray(e); return np.ascontiguousarray(e.reshape(8, -1, 16).transpose(0, 2, 1)).reshape(128, -1).astype(np.int32)
M, Q, V, TOP = 1024, 512, 8, 31
WT = 15
def far_maps(rng):
    p = np.argsort(rng.random((N, 8, M)), axis=-1)
    return np.where(rng.random(p.shape) < 0.125, rng.integers(0, M, p.shape), p).astype(np.int32)
def lists(a):
    return np.stack([gtable(u) for u in a])
def setup_inputs(rng):
    return {"nx": far_maps(rng), "w": rng.integers(0, WT + 1, (N, 8, M)).astype(np.int32), "x": lists(rng.integers(0, M, (N, 8, Q))), "e": lists(rng.integers(0, TOP + 1, (N, 8, V * Q)))}
def setup_inputs_ends(rng):
    d = setup_inputs(rng); k = rng.choice(np.array([0, TOP]), (N, 8, V, Q))
    k[:, :, :, 0] = 0; k[:, :, :, 1] = TOP; k[:, :, :, Q - 1] = 0; k[:, :, V - 1, Q - 1] = TOP
    d["e"] = lists(k.reshape(N, 8, V * Q))
    w = np.where(rng.random((N, 8, M)) < 0.5, WT, 0); w[:, 0] = WT; d["w"] = w.astype(np.int32)
    return d
def setup_inputs_still(rng):
    d = setup_inputs(rng); a = np.array(d["nx"]); s = int(rng.integers(0, 4)); p = np.arange(M)
    for r in range(N):
        h = (r + s) % 4; c = rng.choice(np.arange(2, M - 1), 8, replace=False)
        if h == 0:
            a[r] = p
        elif h == 1:
            c[0] = 0; c[1] = M - 1; a[r] = rng.permutation(c)[:, None]
        elif h == 2:
            c[0] = 1; c[1] = M - 1; a[r] = (p + rng.permutation(c)[:, None]) % M
        else:
            c[0] = 1; c[1] = M - 1; a[r] = p ^ rng.permutation(c)[:, None]
    d["nx"] = a; return d
def setup_inputs_alike(rng):
    d = setup_inputs(rng); k = rng.integers(0, TOP + 1, (N, 8, V, Q // 2))
    z = np.where((np.arange(N)[:, None] + np.arange(8)) % 2 == 0, M - 1, 0)
    d["x"] = lists(np.repeat(z[:, :, None], Q, axis=2)); d["e"] = lists(np.concatenate([k, k], -1).reshape(N, 8, V * Q)); return d
def setup_inputs_spread(rng):
    d = setup_inputs(rng)
    d["nx"] = np.floor(M * rng.random((N, 8, M)) ** 3).astype(np.int32)
    d["w"] = np.floor((WT + 1) * rng.random((N, 8, M)) ** 4).astype(np.int32)
    d["x"] = lists(np.floor(M * rng.random((N, 8, Q)) ** 2)); d["e"] = lists(np.floor((TOP + 1) * rng.random((N, 8, V * Q)) ** 3)); return d
def check_inputs(d):
    bad = []
    for name, top in (("nx", M - 1), ("w", WT), ("x", M - 1), ("e", TOP)):
        if np.min(d[name]) < 0 or np.max(d[name]) > top: bad.append("range of " + name)
    return bad
def reference(nx, w, x, e):
    last = np.zeros((N, 128, Q // 16), np.int32); total = np.zeros((N, 128, Q // 16), np.int32); g = np.arange(8)[:, None]
    for r in range(N):
        p = gentries(x[r]).astype(np.int64); k = gentries(e[r]).reshape(8, V, Q); s = np.zeros((8, Q), np.int64)
        for t in range(V):
            q = (r + t) % N
            for i in range(TOP):
                go = i < k[:, t]
                s = s + np.where(go, w[q][g, p], 0)
                p = np.where(go, nx[q][g, p], p)
        last[r] = gtable(p); total[r] = gtable(s)
    return {"last": np.asarray(last, np.float32), "total": np.asarray(total, np.float32)}

@@ -1,0 +1,363 @@
+from concourse.bass import DstId, RemoteDMATransfer
+from concourse.mybir import AluOpType, ActivationFunctionType
+
+VA = 576
+VC = 736
+VB = 896
+MAGIC = 1.5 * 2.0 ** 23
+SCRATCH = {"OH": ("sbuf", [128, 32], "float32"), "mk": ("sbuf", [128, 4096], "bfloat16")}
+for _n, _w in (("sm", 16), ("rm", 16), ("se", 32), ("rre", 32), ("sx", 4), ("rx", 4)):
+    SCRATCH[_n] = ("dram", [8, 128, _w], "int32")
+for _n in ("od", "ri"):
+    SCRATCH[_n] = ("dram", [8, 128, 8], "float32")
+for _d, _l in (("int32", "W0:1024 A1:1024 cmp:64 ei:256 xi:32 pc:1 ci:8 da:264 db:264 dr:32"),
+               ("float32", "win:5120 W1:1024 W2:1024 adF:1024 OL:32 OD:32 OT:32 cf:24 R1:224 R2:224"),
+               ("float16", "g1:1024 g2:1024 g3:1024 a16:512 gb:1024 c16:64 y16:64 e16:256 h16:256 x16:32 G0:512 G1:512 K1:128 E1:128 E2:128 B15:128 WI:264 WIe:256 WIo:256 WH:256 W7r:256 WT:256 WT7:256 cst:32 w0:80 w1:80 v0:32 v1:32"),
+               ("uint16", "L1:64 L2:64 L4:64 L8:64 lu0:32 lu:256 off:32")):
+    for _e in _l.split():
+        SCRATCH[_e.split(":")[0]] = ("sbuf", [128, int(_e.split(":")[1])], _d)
+for _n in ("pR0", "pR1", "pM0", "pM1", "pN0", "pN1", "pA0", "pA1"):
+    SCRATCH[_n] = ("psum", [128, 512], "float32")
+SEMAPHORES = ["ld", "own", "ld2", "own2", "am", "ae", "ax", "cl", "wl", "al", "el", "xl", "v", "s", "p", "gi", "ls", "st", "own3", "ar", "fin"]
+
+
+def rank_program(g, core, T, topo):
+    me = T.rank_of(core)
+    if me is None:
+        return
+    V, S, P, Y = g.vector, g.scalar, g.tensor, g.sync
+    A = AluOpType
+    COPY = ActivationFunctionType.Copy
+    N = len(T.cores)
+    others = [(me + d) % N for d in range(1, N)]
+    sem = T.sem
+    cnt = {"v": 0, "s": 0, "p": 0, "gi": 0}
+    seen = {}
+    queues = {"v": V, "s": S, "p": P, "g": g, "y": Y}
+
+    def wait(q, *toks):
+        for name, n in toks:
+            if n > seen.get((q, name), 0):
+                queues[q].wait_ge(sem[name], n)
+                seen[(q, name)] = n
+
+    def done(name, ins):
+        cnt[name] += 1
+        ins.then_inc(sem[name], 1)
+        return (name, cnt[name])
+
+    def copyV(out, in_, *w):
+        wait("v", *w)
+        return done("v", V.tensor_copy(out=out, in_=in_))
+
+    def tsV(out, in0, s1, op0, *w, s2=None, op1=None):
+        wait("v", *w)
+        if op1 is None:
+            return done("v", V.tensor_scalar(out=out, in0=in0, scalar1=s1, scalar2=None, op0=op0))
+        return done("v", V.tensor_scalar(out=out, in0=in0, scalar1=s1, scalar2=s2, op0=op0, op1=op1))
+
+    def ttV(out, in0, in1, op, *w):
+        wait("v", *w)
+        return done("v", V.tensor_tensor(out=out, in0=in0, in1=in1, op=op))
+
+    def copyS(out, in_, *w, scale=1.0, bias=0.0):
+        wait("s", *w)
+        return done("s", S.activation(out=out, in_=in_, func=COPY, bias=bias, scale=scale))
+
+    def mm(out, lhsT, rhs, start, stop, *w):
+        wait("p", *w)
+        ins = P.matmul(out=out, lhsT=lhsT, rhs=rhs, start=start, stop=stop)
+        return done("p", ins) if stop else None
+
+    def fused(src, dst, rsem):
+        tr = []
+        for n, d in enumerate(others):
+            c = T.cores[d]
+            rid, pid, _ = topo.addr(c)
+            eng = topo.engines(core, c)
+            e = eng[(2 * n) % len(eng)]
+            tr.append(RemoteDMATransfer(src=src[d], dst=dst[me], dst_ids=[DstId(rid=rid, pnc=pid)], dma_engine_mask=1 << e, remote_sem=sem[rsem]))
+        g.remote_dma_fused(tr, local_sem=sem.ls)
+
+    mine = slice(16 * me, 16 * me + 16)
+    for q, out, in_, name in ((Y, T.sm[:, 0:64, :], T.nx[:, :], "ld"), (S, T.sm[:, 64:128, :], T.w[:, :], "ld"),
+                              (Y, T.se[:], T.e[:, :], "ld2"), (S, T.sx[:], T.x[:, :], "ld2"),
+                              (Y, T.rm[me, 0:64, :], T.nx[me, :], "own"), (S, T.rm[me, 64:128, :], T.w[me, :], "own"),
+                              (Y, T.rre[me], T.e[mine, :], "own2"), (S, T.rx[me], T.x[mine, :], "own2")):
+        q.dma_start(out=out, in_=in_).then_inc(sem[name], 16)
+
+    k_pc = done("gi", g.iota(T.pc[:, 0:1], [[0, 1]], 0, 1))
+    k_da = done("gi", g.iota(T.da[:], [[1, 264]], 128, -1))
+    g.wait_ge(sem.ld, 32)
+    fused(T.sm, T.rm, "am")
+    g.wait_ge(sem.ld2, 32)
+    fused(T.se, T.rre, "ae")
+    fused(T.sx, T.rx, "ax")
+    k_id = done("gi", g.iota(T.win[:, 0:1024], [[1, 1024]], 0, 0, allow_small_or_imprecise_dtypes=True))
+
+    names = ["he", "ho", "r7", "r15", "R67", "u1", "u2", "u3", "u4", "T", "wc", "w8", "neg"]
+    col = {n: T.cf[:, i:i + 1] for i, n in enumerate(names)}
+    c15, c7, c16b, cn, cn7 = [T.ci[:, i:i + 1] for i in range(5)]
+    k_a1 = done("v", V.memset(T.A1[:], 0))
+    k_w0 = done("v", V.memset(T.W0[:], 0))
+    wait("v", k_pc)
+    tsV(c16b, T.pc[:, 0:1], 16, A.bitwise_and)
+    kc = tsV(c15, T.pc[:, 0:1], 15, A.bitwise_and)
+    kc7 = tsV(c7, T.pc[:, 0:1], 7, A.bitwise_and)
+    k_db = tsV(T.db[:], T.da[:], 127, A.bitwise_and, k_da)
+    tsV(col["he"], c16b, 0.0, A.is_equal, kc)
+    tsV(col["ho"], c16b, 16.0, A.is_equal)
+    tsV(col["r7"], c15, 7.0, A.is_equal)
+    k_mat = tsV(T.WI[:], T.db[:], 0.0, A.is_equal, k_db)
+    I = T.WI[:, 0:128]
+    kr15 = tsV(col["r15"], c15, 15.0, A.is_equal)
+    kr67 = tsV(col["R67"], c7, 6.0, A.is_ge, kc7)
+    wait("v", kr15, kr67)
+    for n, f in (("u1", 2.0), ("u2", 6.0), ("u3", 4.0)):
+        tsV(col[n], col["r15"], f, A.mult, s2=col["R67"], op1=A.add)
+    k = tsV(col["u4"], col["r15"], 8.0, A.mult)
+    k_K1 = tsV(T.K1[:], T.db[:, 2:130], col["u1"], A.is_lt, k)
+    k_B15 = tsV(T.B15[:], T.db[:, 7:135], col["u4"], A.is_lt)
+    tsV(T.E1[:], T.db[:, 6:134], col["u2"], A.is_lt)
+    k_E2 = tsV(T.E2[:], T.db[:, 4:132], col["u3"], A.is_lt)
+    k_T = tsV(col["T"], c15, 8.0, A.is_lt)
+    kk = tsV(T.dr[:], T.db[:, 127:159], 7, A.bitwise_and)
+    k = tsV(cn, c15, -1.0, A.mult, s2=128.0, op1=A.add)
+    kk = tsV(T.OH[:], T.dr[:], 0.0, A.is_equal, kk)
+    k = tsV(cn7, cn, 127, A.bitwise_and, k)
+    tsV(col["wc"], col["T"], 1.0 - 2.0 ** -10, A.mult, k_T, s2=2.0 ** -10, op1=A.add)
+    k_neg = copyV(col["neg"], cn7, k)
+    k_oh = tsV(T.OH[:, 0:1], T.OH[:, 0:1], col["T"], A.mult, kk)
+    k_w8 = tsV(col["w8"], col["T"], 8192.0 - 1024.0, A.mult, s2=1024.0, op1=A.add)
+    kcs = tsV(T.cst[:], T.db[:, 0:32], 0.0, A.mult, s2=-1024.0, op1=A.add)
+
+    copyS(T.WIe[:], T.WI[:, 0:256], k_mat, scale=col["he"])
+    k_wio = copyS(T.WIo[:], T.WI[:, 0:256], scale=col["ho"])
+    k_w7r = copyS(T.W7r[:, 0:255], T.WI[:, 7:262], scale=col["r7"])
+    k_wh = copyS(T.WH[:], T.WI[:, 0:256], scale=1024.0)
+
+    nxl, wl = T.rm[:, 0:64, :], T.rm[:, 64:128, :]
+    for e in (Y, S):
+        e.wait_ge(sem.own, 32)
+        e.wait_ge(sem.am, N - 1)
+    Y.dma_start(out=T.cmp[:], in_=nxl).then_inc(sem.cl, 16)
+    wait("y", k_a1, k_w0)
+    wait("s", k_a1, k_w0)
+    S.dma_start(out=T.A1[14::16, :], in_=wl).then_inc(sem.al, 16)
+    Y.dma_start(out=T.A1[6::16, :], in_=nxl).then_inc(sem.al, 16)
+    S.dma_start(out=T.A1[15::16, :], in_=wl).then_inc(sem.al, 16)
+    Y.dma_start(out=T.W0[7::16, :], in_=nxl).then_inc(sem.wl, 16)
+    S.dma_start(out=T.W0[15::16, :], in_=wl).then_inc(sem.wl, 16)
+    Y.wait_ge(sem.own2, 32)
+    Y.wait_ge(sem.ae, N - 1)
+    Y.dma_start(out=T.ei[:], in_=T.rre[:]).then_inc(sem.el, 16)
+    Y.wait_ge(sem.ax, N - 1)
+    Y.dma_start(out=T.xi[:], in_=T.rx[:]).then_inc(sem.xl, 16)
+
+    wait("v", ("cl", 16))
+    k = copyV(T.c16[:], T.cmp[:])
+    wait("v", k)
+    k = done("v", V.transpose(out=T.y16[:], in_=T.c16[:]))
+    k_wt = tsV(T.WT[:], T.db[:, 0:256], col["neg"], A.is_equal, k_neg, s2=col["wc"], op1=A.mult)
+    wait("p", k, k_wio)
+    for b in range(2):
+        for h0 in range(2):
+            for h in range(2):
+                s = 0 if h == h0 else (112 if h == 1 else 16)
+                c = 32 * b + 16 * h
+                kL = mm(T.pR1[:, 2 * b + h0:64:4], (T.WIe, T.WIo)[h0][:, s:s + 128], T.y16[:, c:c + 16], h == 0, h == 1)
+    wait("s", ("al", 48))
+    if VA > 512:
+        copyS(T.a16[:, 0:VA - 512], T.A1[:, 512:VA], scale=0.0)
+    k_a16 = copyS(T.a16[:, VA - 512:512], T.A1[:, VA:1024])
+    wait("s", ("wl", 32))
+    wait("v", ("al", 48), ("wl", 32))
+    kL1 = copyV(T.L1[:], T.pR1[:, 0:64], kL)
+
+    def relay(out, wide, src, shift, first, *w, last=True):
+        wait("p", *w)
+        for r in range(16):
+            s = (shift - r) % 128
+            k = mm(out, wide[:, s:s + 128], src[:, r::16], first and r == 0, last and r == 15)
+        return k
+
+    pN, pA, pK = (T.pN0, T.pN1), (T.pA0, T.pA1), (T.pM1, T.pM0)
+    H = (slice(0, 512), slice(512, 1024))
+    nA = 1024 - VA
+    kg1v = ttV(T.g1[:, 0:VA], T.W0[:].indirect(T.L1[:, 0:VA // 16]), T.A1[:, 0:VA], A.add, kL1)
+    kg1s = copyS(T.g1[:, VA:1024], T.W0[:].indirect(T.L1[:, VA // 16:64]), kL1)
+    wait("p", k_a16, k_K1, k_B15, k_E2)
+    mm(T.pM0[:, 0:nA], I, T.a16[:, VA - 512:512], True, False)
+    mm(pN[1][:], T.K1[:], T.a16[:], True, False)
+    mm(pA[1][:, 0:VC - 512], T.B15[:], T.a16[:, 0:VC - 512], True, False)
+    ka = mm(T.pM0[:, 0:nA], I, T.g1[:, VA:1024], False, True, kg1s)
+    kr = relay(T.pR0[:, 0:64], T.W7r, T.g1, 0, True, k_w7r, kg1v)
+    ks1 = copyS(T.W1[:, VA:1024], T.pM0[:, 0:nA], ka)
+    kv1 = copyV(T.W1[:, 0:VA], T.g1[:, 0:VA], kg1v)
+    wait("v", ("el", 16))
+    klu0 = copyV(T.lu0[:], T.ei[:, 0:32])
+    kl = copyV(T.L2[:], T.pR0[:, 0:64], kr)
+
+    kn0 = mm(pN[0][:], T.K1[:], T.g1[:, H[0]], True, True)
+    mm(pN[1][:], T.K1[:], T.g1[:, H[1]], False, False)
+    mm(pK[0][:], T.E1[:], T.g1[:, H[0]], True, False)
+    mm(pK[1][:], T.E1[:], T.a16[:], True, False, ks1)
+    mm(pK[1][:], T.E1[:], T.g1[:, H[1]], False, False)
+    kg2v = copyV(T.g2[:, H[0]], T.W1[:].indirect(T.L2[:, 0:32]), kl, ks1, kv1)
+    kg2s = copyS(T.g2[:, H[1]], T.W1[:].indirect(T.L2[:, 32:64]), kl, ks1, kv1)
+    kn1 = mm(pN[1][:], I, T.g2[:, H[1]], False, True, kg2s)
+    kr = relay(T.pR1[:, 0:64], T.W7r, T.g2, 0, True, kL1, kg2v)
+    kw2v = ttV(T.W2[:, H[0]], T.g2[:, H[0]], pN[0][:], A.add, kn0, kg2v)
+    copyS(T.mk[:, 0:128], T.OH[:].indirect(T.lu0[:, 0:8]), klu0, k_oh)
+    kw2s = copyS(T.W2[:, H[1]], pN[1][:], kn1)
+    k_e16 = copyV(T.e16[:], T.ei[:])
+    kl = copyV(T.L4[:], T.pR1[:, 0:64], kr)
+
+    ke0 = mm(pK[0][:], T.E2[:], T.g2[:, H[0]], False, True)
+    ke1 = mm(pK[1][:], T.E2[:], T.g2[:, H[1]], False, True)
+    mm(pA[0][:], T.B15[:], T.g1[:, H[0]], True, False)
+    mm(pA[1][:, 0:VC - 512], T.B15[:], T.g1[:, 512:VC], False, False)
+    mm(pA[0][:], T.B15[:], T.g2[:, H[0]], False, False)
+    mm(pA[1][:, 0:VC - 512], T.B15[:], T.g2[:, 512:VC], False, False)
+    kg3v = copyV(T.g3[:, H[0]], T.W2[:].indirect(T.L4[:, 0:32]), kl, kw2v, kw2s)
+    kg3s = copyS(T.g3[:, H[1]], T.W2[:].indirect(T.L4[:, 32:64]), kl, kw2v, kw2s)
+    kad0 = mm(pA[0][:], T.B15[:], T.g3[:, H[0]], False, True, kg3v)
+    kad1 = mm(pA[1][:, 0:VC - 512], T.B15[:], T.g3[:, 512:VC], False, True, kg3s)
+    kr = relay(T.pR0[:, 0:64], T.W7r, T.g3, 0, True)
+    ttV(T.win[:, 1024:1536], T.g3[:, H[0]], pK[0][:], A.add, ke0, kg3v)
+    kb1 = ttV(T.win[:, 1536:2048], T.g3[:, H[1]], pK[1][:], A.add, ke1, kg3s)
+    kmq = copyS(T.mk[:, 128:256], T.OH[:].indirect(T.lu0[:, 8:16]))
+    k_h16 = copyS(T.h16[:, 0:64], T.ei[:, 0:64], scale=0.125, bias=1024.4375)
+    kx = copyS(T.x16[:], T.xi[:], ("xl", 16))
+    kad = [copyS(T.adF[:, 0:512], pA[0][:], kad0)]
+    kad.append(copyS(T.adF[:, 512:VC], pA[1][:, 0:VC - 512], kad1))
+    kl8 = copyV(T.L8[:], T.pR0[:, 0:64], kr)
+    mm(T.pM0[:, 0:32], T.WH[:, 0:128], T.cst[:], True, False, kcs, k_wh, kb1)
+    mm(T.pM0[:, 0:32], T.WH[:, 0:128], T.h16[:, 0:32], False, False, k_h16)
+    ko = mm(T.pM0[:, 0:32], I, T.x16[:], False, True, kx)
+
+    parts = ((VC, VB), (VB, 1024))
+    free = {(2, 0): (kw2v, kw2s), (3, 0): (kw2s,), (2, 1): (kad[1],), (3, 1): (kad[1],)}
+    kprev = [kb1]
+    for B in range(2, 5):
+        a = 1024 * (B - 1)
+        src = T.win[:, a:a + 1024]
+        banks = [(pN[B % 2], pA[B % 2])[n][:, 0:b - u] for n, (u, b) in enumerate(parts)]
+        cuts = (0, 512, VC) if B == 2 else (0, VC)
+        for u0, u1 in zip(cuts, cuts[1:]):
+            kv = ttV(T.win[:, a + 1024 + u0:a + 1024 + u1], src.indirect(T.L8[:, u0 // 16:u1 // 16]), T.adF[:, u0:u1], A.add, kl8, kad[0] if u1 == 512 else kad[1], *kprev)
+        kg, km, ks = [], [], []
+        for u, b in parts:
+            kg.append(copyS(T.gb[:, u:b], src.indirect(T.L8[:, u // 16:b // 16]), kl8, *kprev))
+        for n, (u, b) in enumerate(parts):
+            mm(banks[n], T.B15[:], T.a16[:, u - 512:b - 512], True, False, *free[B, n])
+            for x in (T.g1, T.g2, T.g3):
+                mm(banks[n], T.B15[:], x[:, u:b], False, False)
+        for n, (u, b) in enumerate(parts):
+            km.append(mm(banks[n], I, T.gb[:, u:b], False, True, kg[n]))
+        for n, (u, b) in enumerate(parts):
+            ks.append(copyS(T.win[:, a + 1024 + u:a + 1024 + b], banks[n], km[n]))
+            free[B + 2, n] = (ks[n],)
+        kprev = [kv, ks[1]]
+        if B == 2:
+            wait("p", k_e16)
+            for t in range(1, 8):
+                s = (128 - 16 * t) % 128
+                kt = mm(T.pM1[:, 32 * t:32 * t + 32], T.WI[:, s:s + 128], T.e16[:, 32 * t:32 * t + 32], True, True)
+            koff0 = copyV(T.off[:], T.pM0[:, 0:32], ko)
+        if B == 3:
+            klu1 = copyV(T.lu[:, 32:64], T.pM1[:, 32:64], kt)
+
+    Gs = (T.G0, T.G1)
+    krel, kgat, kw, kS = {}, {}, {}, {}
+    koff = [koff0, koff0]
+    kmask = {(0, 0): kmq}
+
+    def bank_of(t, z):
+        return ((T.pR0, T.pR1), (T.pM0, T.pM1))[t // 5][z]
+
+    def mask(t, z, k, n=1):
+        l = T.lu0[:, 16 * z:16 * z + 16] if t == 0 else T.lu[:, 32 * t + 16 * z:32 * t + 16 * (z + n)]
+        a = 512 * t + 256 * z
+        kmask[t, z] = kmask[t, z + n - 1] = copyS(T.mk[:, a:a + 256 * n], T.OH[:].indirect(l), k)
+
+    def gather(t, z):
+        if t > 1:
+            wait("v", krel[t - 2, z])
+        c = slice(256 * z, 256 * z + 256)
+        m = T.mk[:, 512 * t + 256 * z:512 * t + 256 * z + 256]
+        kgat[t, z] = ttV(Gs[t % 2][:, c], T.win[:].indirect(T.off[:, 16 * z:16 * z + 16]), m, A.mult, koff[z], kmask[t, z], k_id, *kprev)
+
+    mask(0, 1, klu0)
+    mask(1, 0, klu1)
+    mask(1, 1, klu1)
+    k_h16r = copyS(T.h16[:, 64:256], T.ei[:, 64:256], scale=0.125, bias=1024.4375)
+    gather(0, 0)
+    gather(0, 1)
+    klu = copyV(T.lu[:, 64:256], T.pM1[:, 64:256])
+    mask(2, 0, klu)
+    mask(2, 1, klu)
+    for t in range(3, 8):
+        mask(t, 0, klu, 2)
+    k_wt7 = copyS(T.WT7[:], T.WT[:], k_wt, k_w8, scale=col["w8"])
+    wait("p", k_wt, k_h16)
+    for t in range(7):
+        for z in range(2):
+            o = bank_of(t, z)[:, 16 * (t % 5):16 * (t % 5) + 16]
+            if t == 1:
+                wait("p", k_h16r)
+            if t == 5:
+                wait("p", klu)
+            s, c = (128 - 16 * (t + 1)) % 128, 32 * (t + 1) + 16 * z
+            mm(o, T.WH[:, 0:128], T.cst[:, 0:16], True, False, kl8, koff0, koff[z])
+            mm(o, T.WH[:, s:s + 128], T.h16[:, c:c + 16], False, False)
+            krel[t, z] = relay(o, T.WT, Gs[t % 2][:, 256 * z:256 * z + 256], 112, False, kgat[t, z])
+            koff[z] = copyV(T.off[:, 16 * z:16 * z + 16], o, krel[t, z])
+            gather(t + 1, z)
+            if t in (4, 6):
+                b = slice(80 * z, 80 * z + 80) if t == 4 else slice(160 + 32 * z, 192 + 32 * z)
+                k = copyS(T.R1[:, b], bank_of(t, z)[:, 0:b.stop - b.start], koff[z], bias=MAGIC)
+                kS[t, z] = copyS(T.R2[:, b], T.R1[:, b], k, bias=-MAGIC)
+        if t in (5, 6):
+            for z in range(2):
+                b, w = (slice(80 * z, 80 * z + 80), (T.w0, T.w1)[z]) if t == 5 else (slice(160 + 32 * z, 192 + 32 * z), (T.v0, T.v1)[z])
+                kw[t, z] = ttV(w[:], bank_of(0 if t == 5 else 6, z)[:, 0:b.stop - b.start], T.R2[:, b], A.subtract, kS[4 if t == 5 else 6, z])
+
+    wait("p", k_wt7, *kprev)
+    F = T.pA0
+
+    def earlier(z, w, t0, n, k):
+        for t in range(t0, t0 + n):
+            mm(F[:, 16 * z:16 * z + 16], T.WH[:, 16 * (t + 1):16 * (t + 1) + 128], w[:, 16 * (t - t0):16 * (t - t0) + 16], z == 0 and t == 0, False, k)
+
+    earlier(0, T.w0, 0, 5, kw[5, 0])
+    earlier(1, T.w1, 0, 5, kw[5, 1])
+    relay(F[:, 0:16], T.WT7, Gs[1][:, 0:256], 112, False, kgat[7, 0], last=False)
+    wait("p", kgat[7, 1])
+    for r in range(16):
+        s = (112 - r) % 128
+        kf = mm(F[:, 16:32], T.WT7[:, s:s + 128], Gs[1][:, 256 + r:512:16], False, r == 15)
+        if r == 8:
+            earlier(0, T.v0, 5, 2, kw[6, 0])
+        if r == 12:
+            earlier(1, T.v1, 5, 2, kw[6, 1])
+    k8 = tsV(T.OD[:], F[:, 0:32], 8192.0 * MAGIC, A.add, kf, s2=-8192.0 * MAGIC, op1=A.add)
+    kot = ttV(T.OT[:], F[:, 0:32], T.OD[:], A.subtract, k8)
+    kol = copyS(T.OL[:], T.OD[:], k8, scale=2.0 ** -13)
+
+    wait("y", kot)
+    Y.dma_start(out=T.od[:, 64:128, :], in_=T.OT[:]).then_inc(sem.st, 16)
+    Y.dma_start(out=T.ri[me, 64:128, :], in_=T.OT[mine, :]).then_inc(sem.own3, 16)
+    wait("s", kol)
+    S.dma_start(out=T.od[:, 0:64, :], in_=T.OL[:]).then_inc(sem.st, 16)
+    S.dma_start(out=T.ri[me, 0:64, :], in_=T.OL[mine, :]).then_inc(sem.own3, 16)
+    g.wait_ge(sem.st, 32)
+    fused(T.od, T.ri, "ar")
+    for e in (Y, S):
+        e.wait_ge(sem.own3, 32)
+        e.wait_ge(sem.ar, N - 1)
+    Y.dma_start(out=T.last[:, :], in_=T.ri[:, 0:64, :]).then_inc(sem.fin, 16)
+    S.dma_start(out=T.total[:, :], in_=T.ri[:, 64:128, :]).then_inc(sem.fin, 16)
+    wait("g", ("v", cnt["v"]), ("s", cnt["s"]), ("p", cnt["p"]), ("gi", cnt["gi"]))
+    g.wait_ge(sem.ls, 4 * (N - 1))
+    g.wait_ge(sem.fin, 32)

@@ -1,24 +1,27 @@
 from concourse.bass import DstId, RemoteDMATransfer
 from concourse.mybir import AluOpType, ActivationFunctionType
 
-VA = 576
+VA = 640
+V2 = 576
 VC = 736
 VB = 896
+GA = 3
 MAGIC = 1.5 * 2.0 ** 23
-SCRATCH = {"OH": ("sbuf", [128, 32], "float32"), "mk": ("sbuf", [128, 4096], "bfloat16")}
-for _n, _w in (("sm", 16), ("rm", 16), ("se", 32), ("rre", 32), ("sx", 4), ("rx", 4)):
+SCRATCH = {"OH": ("sbuf", [128, 32], "float32"), "mk": ("sbuf", [128, 4096], "bfloat16"),
+           "Xn": ("sbuf", [128, 8, 16], "int32"), "Xe": ("sbuf", [128, 8, 32], "int32"), "Xx": ("sbuf", [128, 8, 4], "int32"),
+           "E16": ("sbuf", [128, 2, 240], "float16"), "Q": ("sbuf", [128, 2, 128], "float16"),
+           "Wz": ("sbuf", [128, 6, 66], "float16"), "ri": ("dram", [8, 128, 8], "float32")}
+for _n, _w in (("sm", 16), ("rm", 16), ("se", 32), ("sx", 4)):
     SCRATCH[_n] = ("dram", [8, 128, _w], "int32")
-for _n in ("od", "ri"):
-    SCRATCH[_n] = ("dram", [8, 128, 8], "float32")
-for _d, _l in (("int32", "W0:1024 A1:1024 cmp:64 ei:256 xi:32 pc:1 ci:8 da:264 db:264 dr:32"),
-               ("float32", "win:5120 W1:1024 W2:1024 adF:1024 OL:32 OD:32 OT:32 cf:24 R1:224 R2:224"),
-               ("float16", "g1:1024 g2:1024 g3:1024 a16:512 gb:1024 c16:64 y16:64 e16:256 h16:256 x16:32 G0:512 G1:512 K1:128 E1:128 E2:128 B15:128 WI:264 WIe:256 WIo:256 WH:256 W7r:256 WT:256 WT7:256 cst:32 w0:80 w1:80 v0:32 v1:32"),
+for _d, _l in (("int32", "W0:1024 A1:1024 pc:1 ci:8 da:264 db:264 dr:32"),
+               ("float32", "win:5120 W1:1024 W2:1024 adF:1024 O:64 cf:24 R1:192 R2:192"),
+               ("float16", "g1:1024 g2:1024 g3:1024 a16:512 gb:1024 c16:128 h16:256 G0:512 G1:512 K1:128 E1:128 E2:128 B15:128 WI:264 WH:128 W7r:256 WT:256 RP:16 RS:16 cst:32 zr:64 Z:144"),
                ("uint16", "L1:64 L2:64 L4:64 L8:64 lu0:32 lu:256 off:32")):
     for _e in _l.split():
         SCRATCH[_e.split(":")[0]] = ("sbuf", [128, int(_e.split(":")[1])], _d)
 for _n in ("pR0", "pR1", "pM0", "pM1", "pN0", "pN1", "pA0", "pA1"):
     SCRATCH[_n] = ("psum", [128, 512], "float32")
-SEMAPHORES = ["ld", "own", "ld2", "own2", "am", "ae", "ax", "cl", "wl", "al", "el", "xl", "v", "s", "p", "gi", "ls", "st", "own3", "ar", "fin"]
+SEMAPHORES = ["ld", "own", "ld2", "ld3", "am", "ae", "ax", "cl", "wl", "al", "v", "s", "p", "gi", "ls", "ar", "fin"]
 
 
 def rank_program(g, core, T, topo):
@@ -64,50 +67,53 @@ def rank_program(g, core, T, topo):
         wait("s", *w)
         return done("s", S.activation(out=out, in_=in_, func=COPY, bias=bias, scale=scale))
 
+    def copyG(out, in_, n, *w):
+        wait("g", *w)
+        return done("gi", g.affine_select(out, in_, [[0, n]], A.is_ge, 0.0, 0, 0))
+
+    def zeroG(out, n):
+        return done("gi", g.affine_select(out, T.WI[:, 0:n], [[0, n]], A.is_gt, 0.0, 0, 0))
+
     def mm(out, lhsT, rhs, start, stop, *w):
         wait("p", *w)
         ins = P.matmul(out=out, lhsT=lhsT, rhs=rhs, start=start, stop=stop)
         return done("p", ins) if stop else None
 
-    def fused(src, dst, rsem):
+    def fused(src, dst, rsem, ks):
         tr = []
         for n, d in enumerate(others):
             c = T.cores[d]
             rid, pid, _ = topo.addr(c)
             eng = topo.engines(core, c)
-            e = eng[(2 * n) % len(eng)]
-            tr.append(RemoteDMATransfer(src=src[d], dst=dst[me], dst_ids=[DstId(rid=rid, pnc=pid)], dma_engine_mask=1 << e, remote_sem=sem[rsem]))
+            m = sum(1 << eng[(2 * n + j) % len(eng)] for j in ks)
+            tr.append(RemoteDMATransfer(src=src(d), dst=dst, dst_ids=[DstId(rid=rid, pnc=pid)], dma_engine_mask=m, remote_sem=sem[rsem]))
         g.remote_dma_fused(tr, local_sem=sem.ls)
 
     mine = slice(16 * me, 16 * me + 16)
+    both = 16 + 2 * (N - 1)
     for q, out, in_, name in ((Y, T.sm[:, 0:64, :], T.nx[:, :], "ld"), (S, T.sm[:, 64:128, :], T.w[:, :], "ld"),
-                              (Y, T.se[:], T.e[:, :], "ld2"), (S, T.sx[:], T.x[:, :], "ld2"),
+                              (Y, T.se[:], T.e[:, :], "ld2"), (S, T.sx[:], T.x[:, :], "ld3"),
                               (Y, T.rm[me, 0:64, :], T.nx[me, :], "own"), (S, T.rm[me, 64:128, :], T.w[me, :], "own"),
-                              (Y, T.rre[me], T.e[mine, :], "own2"), (S, T.rx[me], T.x[mine, :], "own2")):
+                              (Y, T.Xn[0:64, me, :], T.nx[me, :], "cl"),
+                              (Y, T.Xe[:, me, :], T.e[mine, :], "ae"), (S, T.Xx[:, me, :], T.x[mine, :], "ax")):
         q.dma_start(out=out, in_=in_).then_inc(sem[name], 16)
 
     k_pc = done("gi", g.iota(T.pc[:, 0:1], [[0, 1]], 0, 1))
     k_da = done("gi", g.iota(T.da[:], [[1, 264]], 128, -1))
     g.wait_ge(sem.ld, 32)
-    fused(T.sm, T.rm, "am")
-    g.wait_ge(sem.ld2, 32)
-    fused(T.se, T.rre, "ae")
-    fused(T.sx, T.rx, "ax")
+    fused(lambda d: T.sm[d], T.rm[me], "am", (0,))
+    fused(lambda d: T.sm[d], T.Xn[:, me, :], "cl", (0, 1))
     k_id = done("gi", g.iota(T.win[:, 0:1024], [[1, 1024]], 0, 0, allow_small_or_imprecise_dtypes=True))
 
-    names = ["he", "ho", "r7", "r15", "R67", "u1", "u2", "u3", "u4", "T", "wc", "w8", "neg"]
+    names = ["r7", "r15", "R67", "u1", "u2", "u3", "u4", "T", "wc", "nT", "neg"]
     col = {n: T.cf[:, i:i + 1] for i, n in enumerate(names)}
-    c15, c7, c16b, cn, cn7 = [T.ci[:, i:i + 1] for i in range(5)]
+    c15, c7, cn, cn7 = [T.ci[:, i:i + 1] for i in range(4)]
     k_a1 = done("v", V.memset(T.A1[:], 0))
     k_w0 = done("v", V.memset(T.W0[:], 0))
-    wait("v", k_pc)
-    tsV(c16b, T.pc[:, 0:1], 16, A.bitwise_and)
-    kc = tsV(c15, T.pc[:, 0:1], 15, A.bitwise_and)
+    kc = tsV(c15, T.pc[:, 0:1], 15, A.bitwise_and, k_pc)
     kc7 = tsV(c7, T.pc[:, 0:1], 7, A.bitwise_and)
     k_db = tsV(T.db[:], T.da[:], 127, A.bitwise_and, k_da)
-    tsV(col["he"], c16b, 0.0, A.is_equal, kc)
-    tsV(col["ho"], c16b, 16.0, A.is_equal)
-    tsV(col["r7"], c15, 7.0, A.is_equal)
+    tsV(col["r7"], c15, 7.0, A.is_equal, kc)
     k_mat = tsV(T.WI[:], T.db[:], 0.0, A.is_equal, k_db)
     I = T.WI[:, 0:128]
     kr15 = tsV(col["r15"], c15, 15.0, A.is_equal)
@@ -121,26 +127,25 @@ def rank_program(g, core, T, topo):
     tsV(T.E1[:], T.db[:, 6:134], col["u2"], A.is_lt)
     k_E2 = tsV(T.E2[:], T.db[:, 4:132], col["u3"], A.is_lt)
     k_T = tsV(col["T"], c15, 8.0, A.is_lt)
+    tsV(col["nT"], c15, 8.0, A.is_ge)
     kk = tsV(T.dr[:], T.db[:, 127:159], 7, A.bitwise_and)
     k = tsV(cn, c15, -1.0, A.mult, s2=128.0, op1=A.add)
     kk = tsV(T.OH[:], T.dr[:], 0.0, A.is_equal, kk)
     k = tsV(cn7, cn, 127, A.bitwise_and, k)
-    tsV(col["wc"], col["T"], 1.0 - 2.0 ** -10, A.mult, k_T, s2=2.0 ** -10, op1=A.add)
+    kwc = tsV(col["wc"], col["T"], 1.0 - 2.0 ** -10, A.mult, k_T, s2=2.0 ** -10, op1=A.add)
     k_neg = copyV(col["neg"], cn7, k)
     k_oh = tsV(T.OH[:, 0:1], T.OH[:, 0:1], col["T"], A.mult, kk)
-    k_w8 = tsV(col["w8"], col["T"], 8192.0 - 1024.0, A.mult, s2=1024.0, op1=A.add)
     kcs = tsV(T.cst[:], T.db[:, 0:32], 0.0, A.mult, s2=-1024.0, op1=A.add)
+    tsV(T.WT[:], T.db[:, 0:256], col["neg"], A.is_equal, k_neg, kwc, s2=col["wc"], op1=A.mult)
 
-    copyS(T.WIe[:], T.WI[:, 0:256], k_mat, scale=col["he"])
-    k_wio = copyS(T.WIo[:], T.WI[:, 0:256], scale=col["ho"])
-    k_w7r = copyS(T.W7r[:, 0:255], T.WI[:, 7:262], scale=col["r7"])
-    k_wh = copyS(T.WH[:], T.WI[:, 0:256], scale=1024.0)
+    k_w7r = copyS(T.W7r[:, 0:255], T.WI[:, 7:262], k_mat, scale=col["r7"])
+    k_wh = copyS(T.WH[:], I, scale=1024.0)
+    copyS(T.a16[:, 0:VA - 512], T.WI[:, 0:VA - 512], scale=0.0)
 
     nxl, wl = T.rm[:, 0:64, :], T.rm[:, 64:128, :]
     for e in (Y, S):
         e.wait_ge(sem.own, 32)
         e.wait_ge(sem.am, N - 1)
-    Y.dma_start(out=T.cmp[:], in_=nxl).then_inc(sem.cl, 16)
     wait("y", k_a1, k_w0)
     wait("s", k_a1, k_w0)
     S.dma_start(out=T.A1[14::16, :], in_=wl).then_inc(sem.al, 16)
@@ -148,31 +153,32 @@ def rank_program(g, core, T, topo):
     S.dma_start(out=T.A1[15::16, :], in_=wl).then_inc(sem.al, 16)
     Y.dma_start(out=T.W0[7::16, :], in_=nxl).then_inc(sem.wl, 16)
     S.dma_start(out=T.W0[15::16, :], in_=wl).then_inc(sem.wl, 16)
-    Y.wait_ge(sem.own2, 32)
-    Y.wait_ge(sem.ae, N - 1)
-    Y.dma_start(out=T.ei[:], in_=T.rre[:]).then_inc(sem.el, 16)
-    Y.wait_ge(sem.ax, N - 1)
-    Y.dma_start(out=T.xi[:], in_=T.rx[:]).then_inc(sem.xl, 16)
 
-    wait("v", ("cl", 16))
-    k = copyV(T.c16[:], T.cmp[:])
-    wait("v", k)
-    k = done("v", V.transpose(out=T.y16[:], in_=T.c16[:]))
-    k_wt = tsV(T.WT[:], T.db[:, 0:256], col["neg"], A.is_equal, k_neg, s2=col["wc"], op1=A.mult)
-    wait("p", k, k_wio)
+    wait("g", ("ld2", 16), ("ld3", 16), ("al", 48), ("wl", 32))
+    fused(lambda d: T.se[d], T.Xe[:, me, :], "ae", (0, 1))
+    fused(lambda d: T.sx[d], T.Xx[:, me, :], "ax", (0, 1))
+    wait("g", k_mat)
+    k_z = zeroG(T.Z[:], 144)
+    k_zr = zeroG(T.zr[:], 64)
+    for h in range(2):
+        k_e0 = copyG(T.E16[:, h, 0:128], T.Xe[:, :, 16 * h:16 * h + 16], 128, ("ae", both))
+    for h in range(2):
+        k_e1 = copyG(T.E16[:, h, 128:240], T.Xe[:, 0:7, 16 * h:16 * h + 16], 112)
+    for i in range(4):
+        kx = copyG(T.Z[:, 12 + i:140:16], T.Xx[:, :, i], 8, ("ax", both), k_z)
+    zeroG(T.Wz[:, 0:3, :], 198)
+    k_wz = zeroG(T.Wz[:, 3:6, :], 198)
+    wait("g", k_zr)
     for b in range(2):
-        for h0 in range(2):
-            for h in range(2):
-                s = 0 if h == h0 else (112 if h == 1 else 16)
-                c = 32 * b + 16 * h
-                kL = mm(T.pR1[:, 2 * b + h0:64:4], (T.WIe, T.WIo)[h0][:, s:s + 128], T.y16[:, c:c + 16], h == 0, h == 1)
-    wait("s", ("al", 48))
-    if VA > 512:
-        copyS(T.a16[:, 0:VA - 512], T.A1[:, 512:VA], scale=0.0)
-    k_a16 = copyS(T.a16[:, VA - 512:512], T.A1[:, VA:1024])
+        for u in range(2):
+            k_q = done("gi", g.affine_select(T.Q[:, b, 64 * u:64 * u + 64], T.zr[:], [[-16, 8], [-1, 8]], A.not_equal, 1024.0, -8 * b, 1))
+
+    k = copyV(T.c16[0:64, :], T.Xn[0:64, :, :], ("cl", both))
+    kL = mm(T.pR1[:, 0:64], T.c16[0:64, :], T.WI[0:64, 0:64], True, True, k, k_mat)
+    k_a16 = copyS(T.a16[:, VA - 512:512], T.A1[:, VA:1024], ("al", 48))
     wait("s", ("wl", 32))
-    wait("v", ("al", 48), ("wl", 32))
     kL1 = copyV(T.L1[:], T.pR1[:, 0:64], kL)
+    wait("v", ("al", 48), ("wl", 32))
 
     def relay(out, wide, src, shift, first, *w, last=True):
         wait("p", *w)
@@ -181,60 +187,64 @@ def rank_program(g, core, T, topo):
             k = mm(out, wide[:, s:s + 128], src[:, r::16], first and r == 0, last and r == 15)
         return k
 
+    def turned(out, t, *w):
+        s = (N - t) % N
+        for h in range(2):
+            k = mm(out[:, h::2], T.E16[:, h, 16 * s:16 * s + 128], T.WI[:, t:128:8], h == 0, h == 1, *w)
+        return k
+
     pN, pA, pK = (T.pN0, T.pN1), (T.pA0, T.pA1), (T.pM1, T.pM0)
     H = (slice(0, 512), slice(512, 1024))
     nA = 1024 - VA
     kg1v = ttV(T.g1[:, 0:VA], T.W0[:].indirect(T.L1[:, 0:VA // 16]), T.A1[:, 0:VA], A.add, kL1)
     kg1s = copyS(T.g1[:, VA:1024], T.W0[:].indirect(T.L1[:, VA // 16:64]), kL1)
     wait("p", k_a16, k_K1, k_B15, k_E2)
-    mm(T.pM0[:, 0:nA], I, T.a16[:, VA - 512:512], True, False)
+    mm(T.pA0[:, 0:nA], I, T.a16[:, VA - 512:512], True, False)
     mm(pN[1][:], T.K1[:], T.a16[:], True, False)
     mm(pA[1][:, 0:VC - 512], T.B15[:], T.a16[:, 0:VC - 512], True, False)
-    ka = mm(T.pM0[:, 0:nA], I, T.g1[:, VA:1024], False, True, kg1s)
+    mm(pK[1][:], T.E1[:], T.a16[:], True, False)
+    ka = mm(T.pA0[:, 0:nA], I, T.g1[:, VA:1024], False, True, kg1s)
     kr = relay(T.pR0[:, 0:64], T.W7r, T.g1, 0, True, k_w7r, kg1v)
-    ks1 = copyS(T.W1[:, VA:1024], T.pM0[:, 0:nA], ka)
+    ks1 = copyS(T.W1[:, VA:1024], T.pA0[:, 0:nA], ka)
     kv1 = copyV(T.W1[:, 0:VA], T.g1[:, 0:VA], kg1v)
-    wait("v", ("el", 16))
-    klu0 = copyV(T.lu0[:], T.ei[:, 0:32])
     kl = copyV(T.L2[:], T.pR0[:, 0:64], kr)
 
     kn0 = mm(pN[0][:], T.K1[:], T.g1[:, H[0]], True, True)
     mm(pN[1][:], T.K1[:], T.g1[:, H[1]], False, False)
     mm(pK[0][:], T.E1[:], T.g1[:, H[0]], True, False)
-    mm(pK[1][:], T.E1[:], T.a16[:], True, False, ks1)
     mm(pK[1][:], T.E1[:], T.g1[:, H[1]], False, False)
-    kg2v = copyV(T.g2[:, H[0]], T.W1[:].indirect(T.L2[:, 0:32]), kl, ks1, kv1)
-    kg2s = copyS(T.g2[:, H[1]], T.W1[:].indirect(T.L2[:, 32:64]), kl, ks1, kv1)
-    kn1 = mm(pN[1][:], I, T.g2[:, H[1]], False, True, kg2s)
+    mm(pA[1][:, 0:VC - 512], T.B15[:], T.g1[:, 512:VC], False, False)
+    kg2x = copyV(T.g2[:, 512:V2], T.W1[:].indirect(T.L2[:, 32:V2 // 16]), kl, ks1, kv1)
+    kg2v = copyV(T.g2[:, H[0]], T.W1[:].indirect(T.L2[:, 0:32]))
+    kg2s = copyS(T.g2[:, V2:1024], T.W1[:].indirect(T.L2[:, V2 // 16:64]), kl, ks1, kv1)
+    kn1 = mm(pN[1][:], I, T.g2[:, H[1]], False, True, kg2s, kg2x)
     kr = relay(T.pR1[:, 0:64], T.W7r, T.g2, 0, True, kL1, kg2v)
     kw2v = ttV(T.W2[:, H[0]], T.g2[:, H[0]], pN[0][:], A.add, kn0, kg2v)
-    copyS(T.mk[:, 0:128], T.OH[:].indirect(T.lu0[:, 0:8]), klu0, k_oh)
+    tsV(T.RP[:], T.db[:, 0:256:16], col["neg"], A.is_equal, s2=col["T"], op1=A.mult)
     kw2s = copyS(T.W2[:, H[1]], pN[1][:], kn1)
-    k_e16 = copyV(T.e16[:], T.ei[:])
     kl = copyV(T.L4[:], T.pR1[:, 0:64], kr)
 
     ke0 = mm(pK[0][:], T.E2[:], T.g2[:, H[0]], False, True)
     ke1 = mm(pK[1][:], T.E2[:], T.g2[:, H[1]], False, True)
-    mm(pA[0][:], T.B15[:], T.g1[:, H[0]], True, False)
-    mm(pA[1][:, 0:VC - 512], T.B15[:], T.g1[:, 512:VC], False, False)
+    kt0 = turned(T.pR0[:, 64:96], 0, k_e0)
+    mm(pA[0][:], T.B15[:], T.g1[:, H[0]], True, False, ks1)
     mm(pA[0][:], T.B15[:], T.g2[:, H[0]], False, False)
     mm(pA[1][:, 0:VC - 512], T.B15[:], T.g2[:, 512:VC], False, False)
     kg3v = copyV(T.g3[:, H[0]], T.W2[:].indirect(T.L4[:, 0:32]), kl, kw2v, kw2s)
     kg3s = copyS(T.g3[:, H[1]], T.W2[:].indirect(T.L4[:, 32:64]), kl, kw2v, kw2s)
     kad0 = mm(pA[0][:], T.B15[:], T.g3[:, H[0]], False, True, kg3v)
     kad1 = mm(pA[1][:, 0:VC - 512], T.B15[:], T.g3[:, 512:VC], False, True, kg3s)
-    kr = relay(T.pR0[:, 0:64], T.W7r, T.g3, 0, True)
+    klu0 = copyV(T.lu0[:], T.pR0[:, 64:96], kt0)
+    k_h0 = copyS(T.h16[:, 0:32], T.pR0[:, 64:96], klu0, scale=0.125, bias=1024.4375)
+    kr = relay(T.pR0[:, 0:64], T.W7r, T.g3, 0, True, k_h0)
     ttV(T.win[:, 1024:1536], T.g3[:, H[0]], pK[0][:], A.add, ke0, kg3v)
     kb1 = ttV(T.win[:, 1536:2048], T.g3[:, H[1]], pK[1][:], A.add, ke1, kg3s)
-    kmq = copyS(T.mk[:, 128:256], T.OH[:].indirect(T.lu0[:, 8:16]))
-    k_h16 = copyS(T.h16[:, 0:64], T.ei[:, 0:64], scale=0.125, bias=1024.4375)
-    kx = copyS(T.x16[:], T.xi[:], ("xl", 16))
+    copyS(T.mk[:, 0:128], T.OH[:].indirect(T.lu0[:, 0:8]), k_oh)
     kad = [copyS(T.adF[:, 0:512], pA[0][:], kad0)]
     kad.append(copyS(T.adF[:, 512:VC], pA[1][:, 0:VC - 512], kad1))
     kl8 = copyV(T.L8[:], T.pR0[:, 0:64], kr)
-    mm(T.pM0[:, 0:32], T.WH[:, 0:128], T.cst[:], True, False, kcs, k_wh, kb1)
-    mm(T.pM0[:, 0:32], T.WH[:, 0:128], T.h16[:, 0:32], False, False, k_h16)
-    ko = mm(T.pM0[:, 0:32], I, T.x16[:], False, True, kx)
+    k_wt = tsV(T.RS[:], T.db[:, 0:256:16], col["neg"], A.is_equal, s2=col["nT"], op1=A.mult)
+    wait("p", kb1)
 
     parts = ((VC, VB), (VB, 1024))
     free = {(2, 0): (kw2v, kw2s), (3, 0): (kw2s,), (2, 1): (kad[1],), (3, 1): (kad[1],)}
@@ -253,6 +263,12 @@ def rank_program(g, core, T, topo):
             mm(banks[n], T.B15[:], T.a16[:, u - 512:b - 512], True, False, *free[B, n])
             for x in (T.g1, T.g2, T.g3):
                 mm(banks[n], T.B15[:], x[:, u:b], False, False)
+        if B == 2:
+            for t in (1, 2):
+                kt = turned(T.pR1[:, 64 + 32 * t:96 + 32 * t], t, k_e1)
+        if B == 4:
+            for t in (5, 6, 7):
+                kt = turned(T.pM1[:, 32 * t:32 * t + 32], t)
         for n, (u, b) in enumerate(parts):
             km.append(mm(banks[n], I, T.gb[:, u:b], False, True, kg[n]))
         for n, (u, b) in enumerate(parts):
@@ -260,21 +276,26 @@ def rank_program(g, core, T, topo):
             free[B + 2, n] = (ks[n],)
         kprev = [kv, ks[1]]
         if B == 2:
-            wait("p", k_e16)
-            for t in range(1, 8):
-                s = (128 - 16 * t) % 128
-                kt = mm(T.pM1[:, 32 * t:32 * t + 32], T.WI[:, s:s + 128], T.e16[:, 32 * t:32 * t + 32], True, True)
-            koff0 = copyV(T.off[:], T.pM0[:, 0:32], ko)
+            k_h = copyS(T.h16[:, 32:96], T.pR1[:, 96:160], kt, scale=0.125, bias=1024.4375)
+            for t in (3, 4):
+                turned(T.pM1[:, 32 * t:32 * t + 32], t)
+            klu1 = copyV(T.lu[:, 32:96], T.pR1[:, 96:160], k_h)
         if B == 3:
-            klu1 = copyV(T.lu[:, 32:64], T.pM1[:, 32:64], kt)
+            mm(T.pM0[:, 0:32], T.WH[:], T.cst[:], True, False, kcs, k_wh)
+            mm(T.pM0[:, 0:32], T.WH[:], T.h16[:, 0:32], False, False)
+            for u in range(4):
+                ko = mm(T.pM0[:, 0:32], T.Z[:, 12 - 4 * u:140 - 4 * u], T.WI[:, u:128:4], False, u == 3, kx)
+            kmq = copyS(T.mk[:, 128:256], T.OH[:].indirect(T.lu0[:, 8:16]))
+            koff0 = copyV(T.off[:], T.pM0[:, 0:32], ko)
 
     Gs = (T.G0, T.G1)
     krel, kgat, kw, kS = {}, {}, {}, {}
     koff = [koff0, koff0]
     kmask = {(0, 0): kmq}
+    groups = ((0, GA), (GA, 6))
 
     def bank_of(t, z):
-        return ((T.pR0, T.pR1), (T.pM0, T.pM1))[t // 5][z]
+        return ((T.pR0, T.pR1), (T.pM0, T.pM1))[GA <= t < 6][z]
 
     def mask(t, z, k, n=1):
         l = T.lu0[:, 16 * z:16 * z + 16] if t == 0 else T.lu[:, 32 * t + 16 * z:32 * t + 16 * (z + n)]
@@ -288,76 +309,84 @@ def rank_program(g, core, T, topo):
         m = T.mk[:, 512 * t + 256 * z:512 * t + 256 * z + 256]
         kgat[t, z] = ttV(Gs[t % 2][:, c], T.win[:].indirect(T.off[:, 16 * z:16 * z + 16]), m, A.mult, koff[z], kmask[t, z], k_id, *kprev)
 
+    def whole(n, z, k):
+        t0, t1 = groups[n]
+        b = slice(96 * z + 16 * t0, 96 * z + 16 * t1)
+        k = copyS(T.R1[:, b], bank_of(t0, z)[:, 16 * t0:16 * t1], k, bias=MAGIC)
+        kS[n, z] = copyS(T.R2[:, b], T.R1[:, b], k, bias=-MAGIC)
+
+    def fraction(n, z):
+        t0, t1 = groups[n]
+        kw[n, z] = ttV(T.Wz[:, t0:t1, 32 * z + 1:32 * z + 32:2], bank_of(t0, z)[:, 16 * t0:16 * t1], T.R2[:, 96 * z + 16 * t0:96 * z + 16 * t1], A.subtract, kS[n, z], k_wz)
+
+    F = T.pA0
+
+    def earlier(n, ts):
+        for t in ts:
+            for b in range(2):
+                mm(F[64:128, 0:64], T.Wz[:, t, 1 - b:65 - b], T.Q[:, b, 8 * t + 8:8 * t + 72], False, False, kw[n, 0], kw[n, 1], k_q)
+
+    def direct(t, z, kinds, last=False):
+        for u in range(8):
+            for kind in kinds:
+                a = 64 * kind + 32 * z
+                k = mm(F[a:a + 32, u:64:8], Gs[t % 2][:, 256 * z + u:256 * z + 256:8], (T.RP, T.RS)[kind][:, t:t + 8], False,
+                       last and u == 7, kgat[t, z])
+        return k
+
     mask(0, 1, klu0)
     mask(1, 0, klu1)
     mask(1, 1, klu1)
-    k_h16r = copyS(T.h16[:, 64:256], T.ei[:, 64:256], scale=0.125, bias=1024.4375)
     gather(0, 0)
     gather(0, 1)
-    klu = copyV(T.lu[:, 64:256], T.pM1[:, 64:256])
-    mask(2, 0, klu)
-    mask(2, 1, klu)
-    for t in range(3, 8):
+    klu = copyV(T.lu[:, 96:256], T.pM1[:, 96:256], kt)
+    mask(2, 0, klu1)
+    k_h3 = copyS(T.h16[:, 96:256], T.pM1[:, 96:256], klu, scale=0.125, bias=1024.4375)
+    mask(2, 1, klu1)
+    for t in range(3, 6):
         mask(t, 0, klu, 2)
-    k_wt7 = copyS(T.WT7[:], T.WT[:], k_wt, k_w8, scale=col["w8"])
-    wait("p", k_wt, k_h16)
+    wait("p", k_wt, k_h)
+    mm(F[:, 0:64], I, T.zr[:], True, False, k_zr, *kprev)
     for t in range(7):
         for z in range(2):
-            o = bank_of(t, z)[:, 16 * (t % 5):16 * (t % 5) + 16]
-            if t == 1:
-                wait("p", k_h16r)
-            if t == 5:
-                wait("p", klu)
-            s, c = (128 - 16 * (t + 1)) % 128, 32 * (t + 1) + 16 * z
-            mm(o, T.WH[:, 0:128], T.cst[:, 0:16], True, False, kl8, koff0, koff[z])
-            mm(o, T.WH[:, s:s + 128], T.h16[:, c:c + 16], False, False)
+            o = bank_of(t, z)[:, 16 * t:16 * t + 16]
+            if t == 2:
+                wait("p", k_h3)
+            if t == 6:
+                wait("p", kw[0, z])
+            c = 32 * (t + 1) + 16 * z
+            mm(o, T.WH[:], T.cst[:, 0:16], True, False, kl8, klu1, koff0, koff[z])
+            mm(o, T.WH[:], T.h16[:, c:c + 16], False, False)
             krel[t, z] = relay(o, T.WT, Gs[t % 2][:, 256 * z:256 * z + 256], 112, False, kgat[t, z])
             koff[z] = copyV(T.off[:, 16 * z:16 * z + 16], o, krel[t, z])
-            gather(t + 1, z)
             if t in (4, 6):
-                b = slice(80 * z, 80 * z + 80) if t == 4 else slice(160 + 32 * z, 192 + 32 * z)
-                k = copyS(T.R1[:, b], bank_of(t, z)[:, 0:b.stop - b.start], koff[z], bias=MAGIC)
-                kS[t, z] = copyS(T.R2[:, b], T.R1[:, b], k, bias=-MAGIC)
-        if t in (5, 6):
-            for z in range(2):
-                b, w = (slice(80 * z, 80 * z + 80), (T.w0, T.w1)[z]) if t == 5 else (slice(160 + 32 * z, 192 + 32 * z), (T.v0, T.v1)[z])
-                kw[t, z] = ttV(w[:], bank_of(0 if t == 5 else 6, z)[:, 0:b.stop - b.start], T.R2[:, b], A.subtract, kS[4 if t == 5 else 6, z])
+                fraction(t // 6, z)
+            gather(t + 1, z)
+            if t == GA - 1:
+                whole(0, z, koff[z])
+            if t == 5:
+                whole(1, z, koff[z])
+            if 0 <= 2 * t + z - 10 < GA:
+                earlier(0, (2 * t + z - 10,))
+        if t == 2:
+            mask(6, 0, klu, 2)
+            mask(7, 0, klu, 2)
 
-    wait("p", k_wt7, *kprev)
-    F = T.pA0
+    direct(6, 0, (1,))
+    direct(6, 1, (1,))
+    earlier(1, range(GA, 6))
+    direct(7, 0, (0, 1), last=True)
+    kf = direct(7, 1, (0, 1), last=True)
+    kO = copyV(T.O[:], F[:, 0:64], kf)
 
-    def earlier(z, w, t0, n, k):
-        for t in range(t0, t0 + n):
-            mm(F[:, 16 * z:16 * z + 16], T.WH[:, 16 * (t + 1):16 * (t + 1) + 128], w[:, 16 * (t - t0):16 * (t - t0) + 16], z == 0 and t == 0, False, k)
-
-    earlier(0, T.w0, 0, 5, kw[5, 0])
-    earlier(1, T.w1, 0, 5, kw[5, 1])
-    relay(F[:, 0:16], T.WT7, Gs[1][:, 0:256], 112, False, kgat[7, 0], last=False)
-    wait("p", kgat[7, 1])
-    for r in range(16):
-        s = (112 - r) % 128
-        kf = mm(F[:, 16:32], T.WT7[:, s:s + 128], Gs[1][:, 256 + r:512:16], False, r == 15)
-        if r == 8:
-            earlier(0, T.v0, 5, 2, kw[6, 0])
-        if r == 12:
-            earlier(1, T.v1, 5, 2, kw[6, 1])
-    k8 = tsV(T.OD[:], F[:, 0:32], 8192.0 * MAGIC, A.add, kf, s2=-8192.0 * MAGIC, op1=A.add)
-    kot = ttV(T.OT[:], F[:, 0:32], T.OD[:], A.subtract, k8)
-    kol = copyS(T.OL[:], T.OD[:], k8, scale=2.0 ** -13)
-
-    wait("y", kot)
-    Y.dma_start(out=T.od[:, 64:128, :], in_=T.OT[:]).then_inc(sem.st, 16)
-    Y.dma_start(out=T.ri[me, 64:128, :], in_=T.OT[mine, :]).then_inc(sem.own3, 16)
-    wait("s", kol)
-    S.dma_start(out=T.od[:, 0:64, :], in_=T.OL[:]).then_inc(sem.st, 16)
-    S.dma_start(out=T.ri[me, 0:64, :], in_=T.OL[mine, :]).then_inc(sem.own3, 16)
-    g.wait_ge(sem.st, 32)
-    fused(T.od, T.ri, "ar")
+    wait("g", kO)
+    fused(lambda d: T.O[:, 8 * d:8 * d + 8], T.ri[me], "ar", (0, 1))
+    wait("y", kO)
+    Y.dma_start(out=T.ri[me], in_=T.O[:, 8 * me:8 * me + 8]).then_inc(sem.ar, 16)
     for e in (Y, S):
-        e.wait_ge(sem.own3, 32)
-        e.wait_ge(sem.ar, N - 1)
+        e.wait_ge(sem.ar, both)
     Y.dma_start(out=T.last[:, :], in_=T.ri[:, 0:64, :]).then_inc(sem.fin, 16)
     S.dma_start(out=T.total[:, :], in_=T.ri[:, 64:128, :]).then_inc(sem.fin, 16)
     wait("g", ("v", cnt["v"]), ("s", cnt["s"]), ("p", cnt["p"]), ("gi", cnt["gi"]))
-    g.wait_ge(sem.ls, 4 * (N - 1))
+    g.wait_ge(sem.ls, 9 * (N - 1))
     g.wait_ge(sem.fin, 32)

@@ -1,27 +1,27 @@
 from concourse.bass import DstId, RemoteDMATransfer
 from concourse.mybir import AluOpType, ActivationFunctionType
 
-VA = 640
+VA = 608
 V2 = 576
-VC = 736
-VB = 896
-GA = 3
-MAGIC = 1.5 * 2.0 ** 23
+X3 = 256
+W2 = 640
+VC = 640
+VD = 832
+EVEN = (2, 3, 4, 5, 6, 7)
 SCRATCH = {"OH": ("sbuf", [128, 32], "float32"), "mk": ("sbuf", [128, 4096], "bfloat16"),
-           "Xn": ("sbuf", [128, 8, 16], "int32"), "Xe": ("sbuf", [128, 8, 32], "int32"), "Xx": ("sbuf", [128, 8, 4], "int32"),
-           "E16": ("sbuf", [128, 2, 240], "float16"), "Q": ("sbuf", [128, 2, 128], "float16"),
-           "Wz": ("sbuf", [128, 6, 66], "float16"), "ri": ("dram", [8, 128, 8], "float32")}
-for _n, _w in (("sm", 16), ("rm", 16), ("se", 32), ("sx", 4)):
+           "Xn": ("sbuf", [128, 8, 16], "int32"), "Xe": ("sbuf", [128, 8, 32], "int32"), "E16": ("sbuf", [128, 2, 240], "float16"),
+           "ri": ("dram", [8, 128, 8], "float32"), "sm": ("dram", [8, 160, 16], "int32")}
+for _n, _w in (("rm", 16), ("se", 32)):
     SCRATCH[_n] = ("dram", [8, 128, _w], "int32")
 for _d, _l in (("int32", "W0:1024 A1:1024 pc:1 ci:8 da:264 db:264 dr:32"),
-               ("float32", "win:5120 W1:1024 W2:1024 adF:1024 O:64 cf:24 R1:192 R2:192"),
-               ("float16", "g1:1024 g2:1024 g3:1024 a16:512 gb:1024 c16:128 h16:256 G0:512 G1:512 K1:128 E1:128 E2:128 B15:128 WI:264 WH:128 W7r:256 WT:256 RP:16 RS:16 cst:32 zr:64 Z:144"),
-               ("uint16", "L1:64 L2:64 L4:64 L8:64 lu0:32 lu:256 off:32")):
+               ("float32", "win:5120 W1:1024 W2:1024 adF:1024 O:64 cf:24"),
+               ("float16", "g1:1024 g2:1024 g3:1024 a16:512 gb:1024 c16:128 h16:256 G0:512 G1:512 K1:128 E1:128 E2:128 B15:128 WI:264 WH:128 W7r:256 WT:256 R:32 zr:64"),
+               ("uint16", "L1:64 L2:64 L4:64 L8:64 lu:256 off:32")):
     for _e in _l.split():
         SCRATCH[_e.split(":")[0]] = ("sbuf", [128, int(_e.split(":")[1])], _d)
-for _n in ("pR0", "pR1", "pM0", "pM1", "pN0", "pN1", "pA0", "pA1"):
+for _n in ("pR0", "pR1", "pK0", "pK1", "pN0", "pN1", "pA0", "pA1"):
     SCRATCH[_n] = ("psum", [128, 512], "float32")
-SEMAPHORES = ["ld", "own", "ld2", "ld3", "am", "ae", "ax", "cl", "wl", "al", "v", "s", "p", "gi", "ls", "ar", "fin"]
+SEMAPHORES = ["ld", "own", "ld2", "ld3", "am", "ae", "cl", "wl", "al", "v", "s", "p", "gi", "ls", "ar", "fin"]
 
 
 def rank_program(g, core, T, topo):
@@ -67,12 +67,9 @@ def rank_program(g, core, T, topo):
         wait("s", *w)
         return done("s", S.activation(out=out, in_=in_, func=COPY, bias=bias, scale=scale))
 
-    def copyG(out, in_, n, *w):
+    def selG(out, in_, pattern, op, fill, base, cm, *w):
         wait("g", *w)
-        return done("gi", g.affine_select(out, in_, [[0, n]], A.is_ge, 0.0, 0, 0))
-
-    def zeroG(out, n):
-        return done("gi", g.affine_select(out, T.WI[:, 0:n], [[0, n]], A.is_gt, 0.0, 0, 0))
+        return done("gi", g.affine_select(out, in_, pattern, op, fill, base, cm))
 
     def mm(out, lhsT, rhs, start, stop, *w):
         wait("p", *w)
@@ -91,56 +88,44 @@ def rank_program(g, core, T, topo):
 
     mine = slice(16 * me, 16 * me + 16)
     both = 16 + 2 * (N - 1)
-    for q, out, in_, name in ((Y, T.sm[:, 0:64, :], T.nx[:, :], "ld"), (S, T.sm[:, 64:128, :], T.w[:, :], "ld"),
-                              (Y, T.se[:], T.e[:, :], "ld2"), (S, T.sx[:], T.x[:, :], "ld3"),
-                              (Y, T.rm[me, 0:64, :], T.nx[me, :], "own"), (S, T.rm[me, 64:128, :], T.w[me, :], "own"),
-                              (Y, T.Xn[0:64, me, :], T.nx[me, :], "cl"),
-                              (Y, T.Xe[:, me, :], T.e[mine, :], "ae"), (S, T.Xx[:, me, :], T.x[mine, :], "ax")):
+    for q, out, in_, name in ((Y, T.sm[:, 32:96, :], T.nx[:, :], "ld"), (S, T.sm[:, 96:160, :], T.w[:, :], "ld"),
+                              (Y, T.sm[:, 0:32, :], T.x[:, :], "ld3"), (S, T.rm[me, 64:128, :], T.w[me, :], "own"),
+                              (Y, T.rm[me, 0:64, :], T.nx[me, :], "own"), (S, T.Xn[0:32, me, :], T.x[mine, :], "cl"),
+                              (Y, T.Xn[32:96, me, :], T.nx[me, :], "cl"),
+                              (S, T.se[:], T.e[:, :], "ld2"), (Y, T.Xe[:, me, :], T.e[mine, :], "ae")):
         q.dma_start(out=out, in_=in_).then_inc(sem[name], 16)
 
     k_pc = done("gi", g.iota(T.pc[:, 0:1], [[0, 1]], 0, 1))
     k_da = done("gi", g.iota(T.da[:], [[1, 264]], 128, -1))
     g.wait_ge(sem.ld, 32)
-    fused(lambda d: T.sm[d], T.rm[me], "am", (0,))
-    fused(lambda d: T.sm[d], T.Xn[:, me, :], "cl", (0, 1))
+    fused(lambda d: T.sm[d, 32:160, :], T.rm[me], "am", (0,))
+    g.wait_ge(sem.ld3, 16)
+    fused(lambda d: T.sm[d, 0:128, :], T.Xn[:, me, :], "cl", (0, 1))
     k_id = done("gi", g.iota(T.win[:, 0:1024], [[1, 1024]], 0, 0, allow_small_or_imprecise_dtypes=True))
 
-    names = ["r7", "r15", "R67", "u1", "u2", "u3", "u4", "T", "wc", "nT", "neg"]
+    names = ["r7", "r15", "R67", "u1", "u2", "u3", "u4", "T"]
     col = {n: T.cf[:, i:i + 1] for i, n in enumerate(names)}
-    c15, c7, cn, cn7 = [T.ci[:, i:i + 1] for i in range(4)]
+    c15, c7 = [T.ci[:, i:i + 1] for i in range(2)]
     k_a1 = done("v", V.memset(T.A1[:], 0))
     k_w0 = done("v", V.memset(T.W0[:], 0))
     kc = tsV(c15, T.pc[:, 0:1], 15, A.bitwise_and, k_pc)
     kc7 = tsV(c7, T.pc[:, 0:1], 7, A.bitwise_and)
     k_db = tsV(T.db[:], T.da[:], 127, A.bitwise_and, k_da)
     tsV(col["r7"], c15, 7.0, A.is_equal, kc)
-    k_mat = tsV(T.WI[:], T.db[:], 0.0, A.is_equal, k_db)
-    I = T.WI[:, 0:128]
     kr15 = tsV(col["r15"], c15, 15.0, A.is_equal)
     kr67 = tsV(col["R67"], c7, 6.0, A.is_ge, kc7)
+    k_mat = tsV(T.WI[:], T.db[:], 0.0, A.is_equal, k_db)
+    I = T.WI[:, 0:128]
     wait("v", kr15, kr67)
-    for n, f in (("u1", 2.0), ("u2", 6.0), ("u3", 4.0)):
-        tsV(col[n], col["r15"], f, A.mult, s2=col["R67"], op1=A.add)
+    ku = [tsV(col[n], col["r15"], f, A.mult, s2=col["R67"], op1=A.add) for n, f in (("u1", 2.0), ("u2", 6.0), ("u3", 4.0))]
     k = tsV(col["u4"], col["r15"], 8.0, A.mult)
-    k_K1 = tsV(T.K1[:], T.db[:, 2:130], col["u1"], A.is_lt, k)
-    k_B15 = tsV(T.B15[:], T.db[:, 7:135], col["u4"], A.is_lt)
-    tsV(T.E1[:], T.db[:, 6:134], col["u2"], A.is_lt)
-    k_E2 = tsV(T.E2[:], T.db[:, 4:132], col["u3"], A.is_lt)
-    k_T = tsV(col["T"], c15, 8.0, A.is_lt)
-    tsV(col["nT"], c15, 8.0, A.is_ge)
-    kk = tsV(T.dr[:], T.db[:, 127:159], 7, A.bitwise_and)
-    k = tsV(cn, c15, -1.0, A.mult, s2=128.0, op1=A.add)
-    kk = tsV(T.OH[:], T.dr[:], 0.0, A.is_equal, kk)
-    k = tsV(cn7, cn, 127, A.bitwise_and, k)
-    kwc = tsV(col["wc"], col["T"], 1.0 - 2.0 ** -10, A.mult, k_T, s2=2.0 ** -10, op1=A.add)
-    k_neg = copyV(col["neg"], cn7, k)
-    k_oh = tsV(T.OH[:, 0:1], T.OH[:, 0:1], col["T"], A.mult, kk)
-    kcs = tsV(T.cst[:], T.db[:, 0:32], 0.0, A.mult, s2=-1024.0, op1=A.add)
-    tsV(T.WT[:], T.db[:, 0:256], col["neg"], A.is_equal, k_neg, kwc, s2=col["wc"], op1=A.mult)
+    k_K1 = tsV(T.K1[:], T.db[:, 2:130], col["u1"], A.is_lt, ku[0])
+    tsV(T.E1[:], T.db[:, 6:134], col["u2"], A.is_lt, ku[1])
+    tsV(T.E2[:], T.db[:, 4:132], col["u3"], A.is_lt, ku[2])
+    k_B15 = tsV(T.B15[:], T.db[:, 7:135], col["u4"], A.is_lt, k)
 
     k_w7r = copyS(T.W7r[:, 0:255], T.WI[:, 7:262], k_mat, scale=col["r7"])
     k_wh = copyS(T.WH[:], I, scale=1024.0)
-    copyS(T.a16[:, 0:VA - 512], T.WI[:, 0:VA - 512], scale=0.0)
 
     nxl, wl = T.rm[:, 0:64, :], T.rm[:, 64:128, :]
     for e in (Y, S):
@@ -154,229 +139,185 @@ def rank_program(g, core, T, topo):
     Y.dma_start(out=T.W0[7::16, :], in_=nxl).then_inc(sem.wl, 16)
     S.dma_start(out=T.W0[15::16, :], in_=wl).then_inc(sem.wl, 16)
 
-    wait("g", ("ld2", 16), ("ld3", 16), ("al", 48), ("wl", 32))
+    k_zr = selG(T.zr[:], T.WI[:, 0:64], [[0, 64]], A.is_gt, 0.0, 0, 0, k_mat)
+    wait("g", ("ld2", 16), ("al", 48), ("wl", 32))
     fused(lambda d: T.se[d], T.Xe[:, me, :], "ae", (0, 1))
-    fused(lambda d: T.sx[d], T.Xx[:, me, :], "ax", (0, 1))
-    wait("g", k_mat)
-    k_z = zeroG(T.Z[:], 144)
-    k_zr = zeroG(T.zr[:], 64)
-    for h in range(2):
-        k_e0 = copyG(T.E16[:, h, 0:128], T.Xe[:, :, 16 * h:16 * h + 16], 128, ("ae", both))
-    for h in range(2):
-        k_e1 = copyG(T.E16[:, h, 128:240], T.Xe[:, 0:7, 16 * h:16 * h + 16], 112)
-    for i in range(4):
-        kx = copyG(T.Z[:, 12 + i:140:16], T.Xx[:, :, i], 8, ("ax", both), k_z)
-    zeroG(T.Wz[:, 0:3, :], 198)
-    k_wz = zeroG(T.Wz[:, 3:6, :], 198)
-    wait("g", k_zr)
-    for b in range(2):
-        for u in range(2):
-            k_q = done("gi", g.affine_select(T.Q[:, b, 64 * u:64 * u + 64], T.zr[:], [[-16, 8], [-1, 8]], A.not_equal, 1024.0, -8 * b, 1))
+    k = selG(T.R[:], T.zr[:, 0:32], [[8, 2], [0, 2], [16, 8]], A.is_gt, 1.0, 0, -1, k_zr)
+    k_wz = selG(T.WT[:], T.WI[:, 0:256], [[0, 256]], A.is_gt, 0.0, 0, 0)
+    k_R = selG(T.R[:], T.R[:], [[8, 2], [0, 2], [16, 8]], A.is_ge, 0.0, 7, -1, k)
+    for a, b in ((0, 8), (8, 15)):
+        for h in range(2):
+            k_e = selG(T.E16[:, h, 16 * a:16 * b], T.Xe[:, 0:b - a, 16 * h:16 * h + 16], [[0, 16 * (b - a)]], A.is_ge, 0.0, 0, 0, ("ae", both))
+    k_wt = selG(T.WT[:, 0:256:16], T.R[:, 0:16], [[0, 16]], A.is_ge, 0.0, 0, 0, k_wz, k_R)
 
-    k = copyV(T.c16[0:64, :], T.Xn[0:64, :, :], ("cl", both))
-    kL = mm(T.pR1[:, 0:64], T.c16[0:64, :], T.WI[0:64, 0:64], True, True, k, k_mat)
+    k = copyV(T.c16[0:96, :], T.Xn[0:96, :, :], ("cl", both + 16))
+    kL = mm(T.pR1[:, 0:64], T.c16[0:96, :], T.WI[0:96, 32:96], True, True, k, k_mat)
     k_a16 = copyS(T.a16[:, VA - 512:512], T.A1[:, VA:1024], ("al", 48))
     wait("s", ("wl", 32))
+    kk = tsV(T.dr[:], T.db[:, 127:159], 7, A.bitwise_and)
+    k_T = tsV(col["T"], c15, 8.0, A.is_lt)
     kL1 = copyV(T.L1[:], T.pR1[:, 0:64], kL)
+    kk = tsV(T.OH[:], T.dr[:], 0.0, A.is_equal, kk)
     wait("v", ("al", 48), ("wl", 32))
 
-    def relay(out, wide, src, shift, first, *w, last=True):
+    def relay(out, src, *w):
         wait("p", *w)
         for r in range(16):
-            s = (shift - r) % 128
-            k = mm(out, wide[:, s:s + 128], src[:, r::16], first and r == 0, last and r == 15)
+            s = -r % 128
+            k = mm(out, T.W7r[:, s:s + 128], src[:, r::16], r == 0, r == 15)
         return k
 
-    def turned(out, t, *w):
-        s = (N - t) % N
-        for h in range(2):
-            k = mm(out[:, h::2], T.E16[:, h, 16 * s:16 * s + 128], T.WI[:, t:128:8], h == 0, h == 1, *w)
-        return k
-
-    pN, pA, pK = (T.pN0, T.pN1), (T.pA0, T.pA1), (T.pM1, T.pM0)
+    pN, pA, pK = (T.pN0, T.pN1), (T.pA0, T.pA1), (T.pK0, T.pK1)
     H = (slice(0, 512), slice(512, 1024))
     nA = 1024 - VA
     kg1v = ttV(T.g1[:, 0:VA], T.W0[:].indirect(T.L1[:, 0:VA // 16]), T.A1[:, 0:VA], A.add, kL1)
     kg1s = copyS(T.g1[:, VA:1024], T.W0[:].indirect(T.L1[:, VA // 16:64]), kL1)
-    wait("p", k_a16, k_K1, k_B15, k_E2)
+    wait("p", k_a16, k_K1, k_B15)
     mm(T.pA0[:, 0:nA], I, T.a16[:, VA - 512:512], True, False)
-    mm(pN[1][:], T.K1[:], T.a16[:], True, False)
-    mm(pA[1][:, 0:VC - 512], T.B15[:], T.a16[:, 0:VC - 512], True, False)
-    mm(pK[1][:], T.E1[:], T.a16[:], True, False)
+    mm(pN[1][:, W2 - 512:512], T.K1[:], T.a16[:, W2 - 512:512], True, False)
+    mm(pK[1][:, VA - 512:512], T.E1[:], T.a16[:, VA - 512:512], True, False)
+    mm(pA[1][:, VA - 512:VD - 512], T.B15[:], T.a16[:, VA - 512:VD - 512], True, False)
     ka = mm(T.pA0[:, 0:nA], I, T.g1[:, VA:1024], False, True, kg1s)
-    kr = relay(T.pR0[:, 0:64], T.W7r, T.g1, 0, True, k_w7r, kg1v)
+    kr = relay(T.pR0[:, 0:64], T.g1, k_w7r, kg1v)
     ks1 = copyS(T.W1[:, VA:1024], T.pA0[:, 0:nA], ka)
     kv1 = copyV(T.W1[:, 0:VA], T.g1[:, 0:VA], kg1v)
     kl = copyV(T.L2[:], T.pR0[:, 0:64], kr)
+    k_oh = tsV(T.OH[:, 0:1], T.OH[:, 0:1], col["T"], A.mult, kk, k_T)
 
     kn0 = mm(pN[0][:], T.K1[:], T.g1[:, H[0]], True, True)
-    mm(pN[1][:], T.K1[:], T.g1[:, H[1]], False, False)
+    mm(pN[1][:, W2 - 512:512], T.K1[:], T.g1[:, W2:1024], False, False)
     mm(pK[0][:], T.E1[:], T.g1[:, H[0]], True, False)
-    mm(pK[1][:], T.E1[:], T.g1[:, H[1]], False, False)
-    mm(pA[1][:, 0:VC - 512], T.B15[:], T.g1[:, 512:VC], False, False)
-    kg2x = copyV(T.g2[:, 512:V2], T.W1[:].indirect(T.L2[:, 32:V2 // 16]), kl, ks1, kv1)
-    kg2v = copyV(T.g2[:, H[0]], T.W1[:].indirect(T.L2[:, 0:32]))
+    for a, b in ((512, VA), (VA, 1024)):
+        mm(pK[1][:, a - 512:b - 512], T.E1[:], T.g1[:, a:b], False, False)
+    for a, b in ((512, VA), (VA, VD)):
+        mm(pA[1][:, a - 512:b - 512], T.B15[:], T.g1[:, a:b], False, False)
+    mm(T.pR0[:, 0:W2 - 512], T.K1[:], T.g1[:, 512:W2], True, False, kl)
+    knx = mm(T.pR0[:, VA - 512:W2 - 512], T.K1[:], T.a16[:, VA - 512:W2 - 512], False, True)
+    kg2v = copyV(T.g2[:, 0:V2], T.W1[:].indirect(T.L2[:, 0:V2 // 16]), kl, ks1, kv1)
     kg2s = copyS(T.g2[:, V2:1024], T.W1[:].indirect(T.L2[:, V2 // 16:64]), kl, ks1, kv1)
-    kn1 = mm(pN[1][:], I, T.g2[:, H[1]], False, True, kg2s, kg2x)
-    kr = relay(T.pR1[:, 0:64], T.W7r, T.g2, 0, True, kL1, kg2v)
-    kw2v = ttV(T.W2[:, H[0]], T.g2[:, H[0]], pN[0][:], A.add, kn0, kg2v)
-    tsV(T.RP[:], T.db[:, 0:256:16], col["neg"], A.is_equal, s2=col["T"], op1=A.mult)
-    kw2s = copyS(T.W2[:, H[1]], pN[1][:], kn1)
-    kl = copyV(T.L4[:], T.pR1[:, 0:64], kr)
+    kn1 = mm(pN[1][:, W2 - 512:512], I, T.g2[:, W2:1024], False, True, kg2s)
+    kr = relay(T.pR1[:, 0:64], T.g2, kL1, kg2v)
+    ttV(T.W2[:, H[0]], T.g2[:, H[0]], pN[0][:], A.add, kn0, kg2v)
+    kw2v = ttV(T.W2[:, 512:W2], T.g2[:, 512:W2], T.pR0[:, 0:W2 - 512], A.add, knx, kg2s)
+    kw2s = copyS(T.W2[:, W2:1024], pN[1][:, W2 - 512:512], kn1)
+    kl4 = copyV(T.L4[:], T.pR1[:, 0:64], kr)
 
-    ke0 = mm(pK[0][:], T.E2[:], T.g2[:, H[0]], False, True)
+    mm(pK[0][:], T.E2[:], T.g2[:, H[0]], False, False)
+    for o, a, b, k in ((pA[0], 0, X3, ks1), (T.pR1, X3, 512, kl4)):
+        mm(o[:, a:b], T.B15[:], T.g1[:, a:b], True, False, k)
+        mm(o[:, a:b], T.B15[:], T.g2[:, a:b], False, False)
     ke1 = mm(pK[1][:], T.E2[:], T.g2[:, H[1]], False, True)
-    kt0 = turned(T.pR0[:, 64:96], 0, k_e0)
-    mm(pA[0][:], T.B15[:], T.g1[:, H[0]], True, False, ks1)
-    mm(pA[0][:], T.B15[:], T.g2[:, H[0]], False, False)
-    mm(pA[1][:, 0:VC - 512], T.B15[:], T.g2[:, 512:VC], False, False)
-    kg3v = copyV(T.g3[:, H[0]], T.W2[:].indirect(T.L4[:, 0:32]), kl, kw2v, kw2s)
-    kg3s = copyS(T.g3[:, H[1]], T.W2[:].indirect(T.L4[:, 32:64]), kl, kw2v, kw2s)
-    kad0 = mm(pA[0][:], T.B15[:], T.g3[:, H[0]], False, True, kg3v)
-    kad1 = mm(pA[1][:, 0:VC - 512], T.B15[:], T.g3[:, 512:VC], False, True, kg3s)
-    klu0 = copyV(T.lu0[:], T.pR0[:, 64:96], kt0)
-    k_h0 = copyS(T.h16[:, 0:32], T.pR0[:, 64:96], klu0, scale=0.125, bias=1024.4375)
-    kr = relay(T.pR0[:, 0:64], T.W7r, T.g3, 0, True, k_h0)
-    ttV(T.win[:, 1024:1536], T.g3[:, H[0]], pK[0][:], A.add, ke0, kg3v)
-    kb1 = ttV(T.win[:, 1536:2048], T.g3[:, H[1]], pK[1][:], A.add, ke1, kg3s)
-    copyS(T.mk[:, 0:128], T.OH[:].indirect(T.lu0[:, 0:8]), k_oh)
-    kad = [copyS(T.adF[:, 0:512], pA[0][:], kad0)]
+    mm(pA[1][:, 0:VD - 512], T.B15[:], T.g2[:, 512:VD], False, False)
+    kg3v = copyV(T.g3[:, H[1]], T.W2[:].indirect(T.L4[:, 32:64]), kl4, kw2v, kw2s)
+    kx, ky = [copyS(T.g3[:, a:b], T.W2[:].indirect(T.L4[:, a // 16:b // 16]), kl4, kw2v, kw2s) for a, b in ((0, X3), (X3, 512))]
+    ke0 = mm(pK[0][:, 0:X3], I, T.g3[:, 0:X3], False, True, kx)
+    kadx = mm(pA[0][:, 0:X3], T.B15[:], T.g3[:, 0:X3], False, True)
+    kad0 = mm(T.pR1[:, X3:512], T.B15[:], T.g3[:, X3:512], False, True, ky)
+    kr = relay(T.pR0[:, 0:64], T.g3, kg3v, kw2v)
+    kad1 = mm(pA[1][:, 0:VD - 512], T.B15[:], T.g3[:, 512:VD], False, True)
+    kb0 = copyS(T.win[:, 1024:1024 + X3], pK[0][:, 0:X3], ke0)
+    ttV(T.win[:, 1536:2048], T.g3[:, H[1]], pK[1][:], A.add, ke1, kg3v)
+    kb1 = ttV(T.win[:, 1024 + X3:1536], T.g3[:, X3:512], pK[0][:, X3:512], A.add, kb0, ky)
+    kad = [copyS(T.adF[:, 0:X3], pA[0][:, 0:X3], kadx)]
+    copyS(T.adF[:, X3:512], T.pR1[:, X3:512], kad0)
     kad.append(copyS(T.adF[:, 512:VC], pA[1][:, 0:VC - 512], kad1))
     kl8 = copyV(T.L8[:], T.pR0[:, 0:64], kr)
-    k_wt = tsV(T.RS[:], T.db[:, 0:256:16], col["neg"], A.is_equal, s2=col["nT"], op1=A.mult)
-    wait("p", kb1)
 
-    parts = ((VC, VB), (VB, 1024))
-    free = {(2, 0): (kw2v, kw2s), (3, 0): (kw2s,), (2, 1): (kad[1],), (3, 1): (kad[1],)}
-    kprev = [kb1]
+    kmask = {}
+
+    def mask(t, a, b, k):
+        k = copyS(T.mk[:, 512 * t + 128 * a:512 * t + 128 * b], T.OH[:].indirect(T.lu[:, 32 * t + 8 * a:32 * t + 8 * b]), k, k_oh)
+        for i in range(a, b):
+            kmask[t, i] = k
+
+    free = {2: kw2v, 3: kw2s}
+    kprev = [kb0, kb1]
     for B in range(2, 5):
-        a = 1024 * (B - 1)
+        a, u = 1024 * (B - 1), VD
         src = T.win[:, a:a + 1024]
-        banks = [(pN[B % 2], pA[B % 2])[n][:, 0:b - u] for n, (u, b) in enumerate(parts)]
-        cuts = (0, 512, VC) if B == 2 else (0, VC)
+        bank = pN[B % 2][:, 0:1024 - u]
+        cuts = (0, X3, VC) if B == 2 else (0, VC)
         for u0, u1 in zip(cuts, cuts[1:]):
-            kv = ttV(T.win[:, a + 1024 + u0:a + 1024 + u1], src.indirect(T.L8[:, u0 // 16:u1 // 16]), T.adF[:, u0:u1], A.add, kl8, kad[0] if u1 == 512 else kad[1], *kprev)
-        kg, km, ks = [], [], []
-        for u, b in parts:
-            kg.append(copyS(T.gb[:, u:b], src.indirect(T.L8[:, u // 16:b // 16]), kl8, *kprev))
-        for n, (u, b) in enumerate(parts):
-            mm(banks[n], T.B15[:], T.a16[:, u - 512:b - 512], True, False, *free[B, n])
-            for x in (T.g1, T.g2, T.g3):
-                mm(banks[n], T.B15[:], x[:, u:b], False, False)
+            ttV(T.win[:, a + 1024 + u0:a + 1024 + u1], src.indirect(T.L8[:, u0 // 16:u1 // 16]), T.adF[:, u0:u1], A.add, kl8, kad[0] if u1 == X3 else kad[1], *kprev)
+        kg = copyS(T.gb[:, u:1024], src.indirect(T.L8[:, u // 16:64]), kl8, *kprev)
+        kg2 = copyS(T.gb[:, VC:u], src.indirect(T.L8[:, VC // 16:u // 16]))
+        kv = ttV(T.win[:, a + 1024 + VC:a + 1024 + u], T.gb[:, VC:u], pA[1][:, VC - 512:u - 512], A.add, kg2)
+        mm(bank, T.B15[:], T.a16[:, u - 512:512], True, False, free[B])
+        for x in (T.g1, T.g2, T.g3):
+            mm(bank, T.B15[:], x[:, u:1024], False, False)
         if B == 2:
-            for t in (1, 2):
-                kt = turned(T.pR1[:, 64 + 32 * t:96 + 32 * t], t, k_e1)
-        if B == 4:
-            for t in (5, 6, 7):
-                kt = turned(T.pM1[:, 32 * t:32 * t + 32], t)
-        for n, (u, b) in enumerate(parts):
-            km.append(mm(banks[n], I, T.gb[:, u:b], False, True, kg[n]))
-        for n, (u, b) in enumerate(parts):
-            ks.append(copyS(T.win[:, a + 1024 + u:a + 1024 + b], banks[n], km[n]))
-            free[B + 2, n] = (ks[n],)
-        kprev = [kv, ks[1]]
+            wait("p", k_e, kb1)
+            for t in range(8):
+                s = 16 * ((N - t) % N)
+                for h in range(2):
+                    kt = mm(pK[0][:, 32 * t + h:32 * t + 32:2], T.E16[:, h, s:s + 128], T.WI[:, t:128:8], t + h == 0, t + h == 8)
+            k_h = copyS(T.h16[:, 0:64], pK[0][:, 0:64], kt, scale=0.125, bias=1024.4375)
+        km = mm(bank, I, T.gb[:, u:1024], False, True, kg)
+        if B > 2:
+            mask(0, 2 * B - 6, 2 * B - 5, klu)
+        ks = copyS(T.win[:, a + 1024 + u:a + 2048], bank, km)
+        free[B + 2] = ks
+        kprev = [kv, ks]
         if B == 2:
-            k_h = copyS(T.h16[:, 32:96], T.pR1[:, 96:160], kt, scale=0.125, bias=1024.4375)
-            for t in (3, 4):
-                turned(T.pM1[:, 32 * t:32 * t + 32], t)
-            klu1 = copyV(T.lu[:, 32:96], T.pR1[:, 96:160], k_h)
+            klu = copyV(T.lu[:], pK[0][:, 0:256], k_h)
+            mm(pK[1][:, 0:32], T.c16[0:96, :], T.WI[0:96, 0:32], True, False)
+            ko = mm(pK[1][:, 0:32], T.WH[:], T.h16[:, 0:32], False, True, k_h, k_wh)
         if B == 3:
-            mm(T.pM0[:, 0:32], T.WH[:], T.cst[:], True, False, kcs, k_wh)
-            mm(T.pM0[:, 0:32], T.WH[:], T.h16[:, 0:32], False, False)
-            for u in range(4):
-                ko = mm(T.pM0[:, 0:32], T.Z[:, 12 - 4 * u:140 - 4 * u], T.WI[:, u:128:4], False, u == 3, kx)
-            kmq = copyS(T.mk[:, 128:256], T.OH[:].indirect(T.lu0[:, 8:16]))
-            koff0 = copyV(T.off[:], T.pM0[:, 0:32], ko)
+            koff0 = tsV(T.off[:], pK[1][:, 0:32], -2.0 ** 20, A.add, ko)
 
-    Gs = (T.G0, T.G1)
-    krel, kgat, kw, kS = {}, {}, {}, {}
-    koff = [koff0, koff0]
-    kmask = {(0, 0): kmq}
-    groups = ((0, GA), (GA, 6))
-
-    def bank_of(t, z):
-        return ((T.pR0, T.pR1), (T.pM0, T.pM1))[GA <= t < 6][z]
-
-    def mask(t, z, k, n=1):
-        l = T.lu0[:, 16 * z:16 * z + 16] if t == 0 else T.lu[:, 32 * t + 16 * z:32 * t + 16 * (z + n)]
-        a = 512 * t + 256 * z
-        kmask[t, z] = kmask[t, z + n - 1] = copyS(T.mk[:, a:a + 256 * n], T.OH[:].indirect(l), k)
-
-    def gather(t, z):
-        if t > 1:
-            wait("v", krel[t - 2, z])
-        c = slice(256 * z, 256 * z + 256)
-        m = T.mk[:, 512 * t + 256 * z:512 * t + 256 * z + 256]
-        kgat[t, z] = ttV(Gs[t % 2][:, c], T.win[:].indirect(T.off[:, 16 * z:16 * z + 16]), m, A.mult, koff[z], kmask[t, z], k_id, *kprev)
-
-    def whole(n, z, k):
-        t0, t1 = groups[n]
-        b = slice(96 * z + 16 * t0, 96 * z + 16 * t1)
-        k = copyS(T.R1[:, b], bank_of(t0, z)[:, 16 * t0:16 * t1], k, bias=MAGIC)
-        kS[n, z] = copyS(T.R2[:, b], T.R1[:, b], k, bias=-MAGIC)
-
-    def fraction(n, z):
-        t0, t1 = groups[n]
-        kw[n, z] = ttV(T.Wz[:, t0:t1, 32 * z + 1:32 * z + 32:2], bank_of(t0, z)[:, 16 * t0:16 * t1], T.R2[:, 96 * z + 16 * t0:96 * z + 16 * t1], A.subtract, kS[n, z], k_wz)
-
+    krel = {}
+    koff = [koff0] * 4
     F = T.pA0
-
-    def earlier(n, ts):
-        for t in ts:
-            for b in range(2):
-                mm(F[64:128, 0:64], T.Wz[:, t, 1 - b:65 - b], T.Q[:, b, 8 * t + 8:8 * t + 72], False, False, kw[n, 0], kw[n, 1], k_q)
+    Gs = (T.G0, T.G1)
+    banks = (T.pR0, T.pR1, T.pN1, T.pK1)
 
     def direct(t, z, kinds, last=False):
         for u in range(8):
             for kind in kinds:
                 a = 64 * kind + 32 * z
-                k = mm(F[a:a + 32, u:64:8], Gs[t % 2][:, 256 * z + u:256 * z + 256:8], (T.RP, T.RS)[kind][:, t:t + 8], False,
-                       last and u == 7, kgat[t, z])
+                k = mm(F[a:a + 32, u:64:8], Gs[t % 2][:, 256 * z + u:256 * z + 256:8], T.R[:, 16 * kind + t:16 * kind + t + 8], False, last and u == 7)
         return k
 
-    mask(0, 1, klu0)
-    mask(1, 0, klu1)
-    mask(1, 1, klu1)
-    gather(0, 0)
-    gather(0, 1)
-    klu = copyV(T.lu[:, 96:256], T.pM1[:, 96:256], kt)
-    mask(2, 0, klu1)
-    k_h3 = copyS(T.h16[:, 96:256], T.pM1[:, 96:256], klu, scale=0.125, bias=1024.4375)
-    mask(2, 1, klu1)
-    for t in range(3, 6):
-        mask(t, 0, klu, 2)
-    wait("p", k_wt, k_h)
-    mm(F[:, 0:64], I, T.zr[:], True, False, k_zr, *kprev)
-    for t in range(7):
-        for z in range(2):
-            o = bank_of(t, z)[:, 16 * t:16 * t + 16]
-            if t == 2:
-                wait("p", k_h3)
-            if t == 6:
-                wait("p", kw[0, z])
-            c = 32 * (t + 1) + 16 * z
-            mm(o, T.WH[:], T.cst[:, 0:16], True, False, kl8, klu1, koff0, koff[z])
-            mm(o, T.WH[:], T.h16[:, c:c + 16], False, False)
-            krel[t, z] = relay(o, T.WT, Gs[t % 2][:, 256 * z:256 * z + 256], 112, False, kgat[t, z])
-            koff[z] = copyV(T.off[:, 16 * z:16 * z + 16], o, krel[t, z])
-            if t in (4, 6):
-                fraction(t // 6, z)
-            gather(t + 1, z)
-            if t == GA - 1:
-                whole(0, z, koff[z])
-            if t == 5:
-                whole(1, z, koff[z])
-            if 0 <= 2 * t + z - 10 < GA:
-                earlier(0, (2 * t + z - 10,))
-        if t == 2:
-            mask(6, 0, klu, 2)
-            mask(7, 0, klu, 2)
+    def gather(t, i):
+        G, a = Gs[t % 2], 128 * i
+        k = ttV(G[:, a:a + 128], T.win[:].indirect(T.off[:, 8 * i:8 * i + 8]), T.mk[:, 512 * t + a:512 * t + a + 128], A.mult,
+                kmask[t, i], koff[i], k_id, *kprev)
+        if t < 7:
+            o = banks[i][:, 0:8]
+            c = 32 * (t + 1) + 8 * i
+            mm(o, T.WH[:], T.h16[:, c:c + 8], True, False, koff[i], *([k_h2] if t else []))
+            for r in range(16):
+                krel[i] = mm(o, T.WT[:, 112 - r:240 - r], G[:, a + r:a + 128:16], False, r == 15, k)
+        if i % 2:
+            wait("p", k)
+            return direct(t, i // 2, (0, 1) if t == 7 else (1,), last=t == 7)
 
-    direct(6, 0, (1,))
-    direct(6, 1, (1,))
-    earlier(1, range(GA, 6))
-    direct(7, 0, (0, 1), last=True)
-    kf = direct(7, 1, (0, 1), last=True)
+    def offsets(i):
+        koff[i] = tsV(T.off[:, 8 * i:8 * i + 8], banks[i][:, 0:8], -2.0 ** 20, A.add, krel[i])
+
+    mask(0, 1, 2, klu)
+    mask(0, 3, 4, klu)
+    mask(1, 0, 2, klu)
+    k_h2 = copyS(T.h16[:, 64:256], pK[0][:, 64:256], scale=0.125, bias=1024.4375)
+    mask(1, 2, 4, klu)
+    mask(2, 0, 2, klu)
+    mask(2, 2, 4, klu)
+    for t in range(3, 8):
+        mask(t, 0, 4, klu)
+    wait("p", k_wt, kl8, kad[1], klu, k_zr)
+    mm(F[:, 0:64], I, T.zr[:], True, False)
+    for i in range(3):
+        gather(0, i)
+    for t in range(1, 8):
+        if t not in EVEN:
+            gather(t - 1, 3)
+        offsets(0)
+        if t in EVEN:
+            gather(t - 1, 3)
+        for i in range(3):
+            offsets(i + 1)
+            gather(t, i)
+    kf = gather(7, 3)
     kO = copyV(T.O[:], F[:, 0:64], kf)
 
     wait("g", kO)
@@ -388,5 +329,5 @@ def rank_program(g, core, T, topo):
     Y.dma_start(out=T.last[:, :], in_=T.ri[:, 0:64, :]).then_inc(sem.fin, 16)
     S.dma_start(out=T.total[:, :], in_=T.ri[:, 64:128, :]).then_inc(sem.fin, 16)
     wait("g", ("v", cnt["v"]), ("s", cnt["s"]), ("p", cnt["p"]), ("gi", cnt["gi"]))
-    g.wait_ge(sem.ls, 9 * (N - 1))
+    g.wait_ge(sem.ls, 7 * (N - 1))
     g.wait_ge(sem.fin, 32)

@@ -1,27 +1,27 @@
 from concourse.bass import DstId, RemoteDMATransfer
 from concourse.mybir import AluOpType, ActivationFunctionType
 
-VA = 608
-V2 = 576
-X3 = 256
-W2 = 640
-VC = 640
-VD = 832
-EVEN = (2, 3, 4, 5, 6, 7)
-SCRATCH = {"OH": ("sbuf", [128, 32], "float32"), "mk": ("sbuf", [128, 4096], "bfloat16"),
-           "Xn": ("sbuf", [128, 8, 16], "int32"), "Xe": ("sbuf", [128, 8, 32], "int32"), "E16": ("sbuf", [128, 2, 240], "float16"),
-           "ri": ("dram", [8, 128, 8], "float32"), "sm": ("dram", [8, 160, 16], "int32")}
-for _n, _w in (("rm", 16), ("se", 32)):
-    SCRATCH[_n] = ("dram", [8, 128, _w], "int32")
-for _d, _l in (("int32", "W0:1024 A1:1024 pc:1 ci:8 da:264 db:264 dr:32"),
-               ("float32", "win:5120 W1:1024 W2:1024 adF:1024 O:64 cf:24"),
-               ("float16", "g1:1024 g2:1024 g3:1024 a16:512 gb:1024 c16:128 h16:256 G0:512 G1:512 K1:128 E1:128 E2:128 B15:128 WI:264 WH:128 W7r:256 WT:256 R:32 zr:64"),
-               ("uint16", "L1:64 L2:64 L4:64 L8:64 lu:256 off:32")):
+X3 = 224
+M1 = 864
+CS = 640
+V2 = 960
+VC = 384
+VD = 160
+LATE = 24
+MS = ((0, 2), (2, 4), (6, 7), (4, 6), (7, 8), (8, 12), (12, 16), (16, 22), (22, 30), (30, 40), (40, 52), (52, 64))
+SCRATCH = {"OH": ("sbuf", [128, 32], "float32"), "mk": ("sbuf", [128, 4096], "bfloat16"), "Xe": ("sbuf", [128, 8, 32], "int32"),
+           "E16": ("sbuf", [128, 2, 240], "float16"), "Ya": ("sbuf", [128, 130, 16], "bfloat16"),
+           "ri": ("dram", [8, 128, 8], "float32"), "sm": ("dram", [8, 160, 16], "int32"), "se": ("dram", [8, 128, 32], "int32"),
+           "rm": ("dram", [8, 128, 16], "int32")}
+for _d, _l in (("int32", "W0:1024 A1:512 Xn:128 pc:1 ci:8 da:160 idv:64"),
+               ("float32", "win:5120 W1:1024 W2:1024 O:64 cf:24 m1:40 m2:32"),
+               ("float16", "g1:1344 g2:1344 g3:1024 w16:512 ad:1024 gb:512 c16:128 h16:256 G0:512 G1:512 K1:128 E1:128 E2:128 D13:128 WJ:160 WH:128 W7r:144 WT:256 R:32 zr:64"),
+               ("uint16", "L1:64 L2:96 L4:96 L8:64 lu:256 off:32")):
     for _e in _l.split():
         SCRATCH[_e.split(":")[0]] = ("sbuf", [128, int(_e.split(":")[1])], _d)
-for _n in ("pR0", "pR1", "pK0", "pK1", "pN0", "pN1", "pA0", "pA1"):
-    SCRATCH[_n] = ("psum", [128, 512], "float32")
-SEMAPHORES = ["ld", "own", "ld2", "ld3", "am", "ae", "cl", "wl", "al", "v", "s", "p", "gi", "ls", "ar", "fin"]
+for _n in range(8):
+    SCRATCH["b%d" % _n] = ("psum", [128, 512], "float32")
+SEMAPHORES = ["ld", "ld2", "ld3", "own", "am", "cl", "wl", "al", "ae", "v", "s", "p", "gi", "ls", "ar", "fin"]
 
 
 def rank_program(g, core, T, topo):
@@ -37,6 +37,7 @@ def rank_program(g, core, T, topo):
     cnt = {"v": 0, "s": 0, "p": 0, "gi": 0}
     seen = {}
     queues = {"v": V, "s": S, "p": P, "g": g, "y": Y}
+    b0, b1, b2, b3, b4, b5, b6, b7 = [T["b%d" % n] for n in range(8)]
 
     def wait(q, *toks):
         for name, n in toks:
@@ -71,12 +72,15 @@ def rank_program(g, core, T, topo):
         wait("g", *w)
         return done("gi", g.affine_select(out, in_, pattern, op, fill, base, cm))
 
+    def copyG(out, in_, n, *w):
+        return selG(out, in_, [[0, n]], A.is_ge, 0.0, 0, 0, *w)
+
     def mm(out, lhsT, rhs, start, stop, *w):
         wait("p", *w)
         ins = P.matmul(out=out, lhsT=lhsT, rhs=rhs, start=start, stop=stop)
         return done("p", ins) if stop else None
 
-    def fused(src, dst, rsem, ks):
+    def fused(src, dst, rsem, ks=(0, 1)):
         tr = []
         for n, d in enumerate(others):
             c = T.cores[d]
@@ -90,238 +94,268 @@ def rank_program(g, core, T, topo):
     both = 16 + 2 * (N - 1)
     for q, out, in_, name in ((Y, T.sm[:, 32:96, :], T.nx[:, :], "ld"), (S, T.sm[:, 96:160, :], T.w[:, :], "ld"),
                               (Y, T.sm[:, 0:32, :], T.x[:, :], "ld3"), (S, T.rm[me, 64:128, :], T.w[me, :], "own"),
-                              (Y, T.rm[me, 0:64, :], T.nx[me, :], "own"), (S, T.Xn[0:32, me, :], T.x[mine, :], "cl"),
-                              (Y, T.Xn[32:96, me, :], T.nx[me, :], "cl"),
-                              (S, T.se[:], T.e[:, :], "ld2"), (Y, T.Xe[:, me, :], T.e[mine, :], "ae")):
+                              (Y, T.rm[me, 0:64, :], T.nx[me, :], "own"), (S, T.Xn[0:32, mine], T.x[mine, :], "cl"),
+                              (Y, T.Xn[32:96, mine], T.nx[me, :], "cl"), (Y, T.Xn[96:128, mine], T.w[me, 0:512], "cl")):
         q.dma_start(out=out, in_=in_).then_inc(sem[name], 16)
+    landed = ("cl", both + 32)
 
+    k_idv = done("gi", g.iota(T.idv[:], [[1, 64]], 0, 64))
     k_pc = done("gi", g.iota(T.pc[:, 0:1], [[0, 1]], 0, 1))
-    k_da = done("gi", g.iota(T.da[:], [[1, 264]], 128, -1))
+    k_da = done("gi", g.iota(T.da[:], [[1, 160]], -16, -1))
     g.wait_ge(sem.ld, 32)
     fused(lambda d: T.sm[d, 32:160, :], T.rm[me], "am", (0,))
     g.wait_ge(sem.ld3, 16)
-    fused(lambda d: T.sm[d, 0:128, :], T.Xn[:, me, :], "cl", (0, 1))
-    k_id = done("gi", g.iota(T.win[:, 0:1024], [[1, 1024]], 0, 0, allow_small_or_imprecise_dtypes=True))
+    fused(lambda d: T.sm[d, 0:128, :], T.Xn[:, mine], "cl")
+    g.iota(T.m1[:, 0:1], [[0, 1]], 6, 0, allow_small_or_imprecise_dtypes=True)
+    k_m0 = done("gi", g.iota(T.m1[:, 1:33], [[0, 4], [1, 8]], 0, 0, allow_small_or_imprecise_dtypes=True))
 
-    names = ["r7", "r15", "R67", "u1", "u2", "u3", "u4", "T"]
+    names = ["r7", "r12", "r13", "r15", "a14", "c7", "j", "j1", "u0", "u1", "u2"]
     col = {n: T.cf[:, i:i + 1] for i, n in enumerate(names)}
-    c15, c7 = [T.ci[:, i:i + 1] for i in range(2)]
-    k_a1 = done("v", V.memset(T.A1[:], 0))
+    c15 = T.ci[:, 0:1]
+    k_z = done("v", V.memset(T.Ya[:, 0:65, :], 0.0))
+    k_ya = copyS(T.Ya[:, 65:130, :], T.Ya[:, 0:65, :], k_z)
+    k_idl = tsV(T.idv[:], T.idv[:], 1023, A.bitwise_and, k_idv)
     k_w0 = done("v", V.memset(T.W0[:], 0))
     kc = tsV(c15, T.pc[:, 0:1], 15, A.bitwise_and, k_pc)
-    kc7 = tsV(c7, T.pc[:, 0:1], 7, A.bitwise_and)
-    k_db = tsV(T.db[:], T.da[:], 127, A.bitwise_and, k_da)
+    wait("y", k_w0, k_idl)
+    Y.dma_start(out=T.W0[6::16, :], in_=T.idv[:]).then_inc(sem.wl, 16)
+    Y.dma_start(out=T.se[:], in_=T.e[:, :]).then_inc(sem.ld2, 16)
+    Y.dma_start(out=T.Xe[:, me, :], in_=T.e[mine, :]).then_inc(sem.ae, 16)
+    k_a1 = done("v", V.memset(T.A1[:], 0))
     tsV(col["r7"], c15, 7.0, A.is_equal, kc)
-    kr15 = tsV(col["r15"], c15, 15.0, A.is_equal)
-    kr67 = tsV(col["R67"], c7, 6.0, A.is_ge, kc7)
-    k_mat = tsV(T.WI[:], T.db[:], 0.0, A.is_equal, k_db)
-    I = T.WI[:, 0:128]
-    wait("v", kr15, kr67)
-    ku = [tsV(col[n], col["r15"], f, A.mult, s2=col["R67"], op1=A.add) for n, f in (("u1", 2.0), ("u2", 6.0), ("u3", 4.0))]
-    k = tsV(col["u4"], col["r15"], 8.0, A.mult)
-    k_K1 = tsV(T.K1[:], T.db[:, 2:130], col["u1"], A.is_lt, ku[0])
-    tsV(T.E1[:], T.db[:, 6:134], col["u2"], A.is_lt, ku[1])
-    tsV(T.E2[:], T.db[:, 4:132], col["u3"], A.is_lt, ku[2])
-    k_B15 = tsV(T.B15[:], T.db[:, 7:135], col["u4"], A.is_lt, k)
+    tsV(col["r13"], c15, 13.0, A.is_equal)
+    tsV(col["r15"], c15, 15.0, A.is_equal)
+    tsV(col["a14"], c15, 14.0, A.is_ge)
+    tsV(col["u1"], c15, 14.0, A.is_equal, s2=201.0, op1=A.mult)
+    k_mat = tsV(T.WJ[:], T.da[:], 0.0, A.is_equal, k_da)
+    I = T.WJ[:, 16:144]
 
-    k_w7r = copyS(T.W7r[:, 0:255], T.WI[:, 7:262], k_mat, scale=col["r7"])
-    k_wh = copyS(T.WH[:], I, scale=1024.0)
-
-    nxl, wl = T.rm[:, 0:64, :], T.rm[:, 64:128, :]
     for e in (Y, S):
         e.wait_ge(sem.own, 32)
         e.wait_ge(sem.am, N - 1)
-    wait("y", k_a1, k_w0)
-    wait("s", k_a1, k_w0)
-    S.dma_start(out=T.A1[14::16, :], in_=wl).then_inc(sem.al, 16)
-    Y.dma_start(out=T.A1[6::16, :], in_=nxl).then_inc(sem.al, 16)
-    S.dma_start(out=T.A1[15::16, :], in_=wl).then_inc(sem.al, 16)
-    Y.dma_start(out=T.W0[7::16, :], in_=nxl).then_inc(sem.wl, 16)
-    S.dma_start(out=T.W0[15::16, :], in_=wl).then_inc(sem.wl, 16)
+    wait("y", k_a1)
+    wait("s", k_a1)
+    wtop = T.rm[:, 96:128, :]
+    Y.dma_start(out=T.W0[7::8, :], in_=T.rm[:]).then_inc(sem.wl, 16)
+    S.dma_start(out=T.W0[13::16, :], in_=T.rm[:, 64:128, :]).then_inc(sem.wl, 16)
+    Y.dma_start(out=T.A1[13::16, :], in_=wtop).then_inc(sem.al, 16)
+    S.dma_start(out=T.A1[14::16, :], in_=wtop).then_inc(sem.al, 16)
+    inlanes, added = ("wl", 48), ("al", 32)
+    k_w7r = copyS(T.W7r[:], T.WJ[:, 8:152], k_mat, scale=col["r7"])
+    k_d13 = copyS(T.D13[:], I, scale=col["r13"])
+    k_wh = copyS(T.WH[:], I, scale=1024.0)
 
-    k_zr = selG(T.zr[:], T.WI[:, 0:64], [[0, 64]], A.is_gt, 0.0, 0, 0, k_mat)
-    wait("g", ("ld2", 16), ("al", 48), ("wl", 32))
-    fused(lambda d: T.se[d], T.Xe[:, me, :], "ae", (0, 1))
+    def lanes(bank, a, b, s, stop, *w):
+        wait("p", *w)
+        for r in range(16):
+            k = mm(bank[:, r:b - a:16], T.Ya[96:128, s:s + 128, r], T.WJ[96:128, 112 + a // 16:112 + b // 16], r == 0, stop and r == 15)
+        return k
+
+    def relay(bank, src, a, b, start, stop, *w):
+        wait("p", *w)
+        for r in range(16):
+            k = mm(bank[:, a // 16:b // 16], T.W7r[:, 15 - r:143 - r], src[:, a + r:b:16], start and r == 0, stop and r == 15)
+        return k
+
+    tsV(col["u0"], col["r13"], col["r15"], A.subtract, k_mat, s2=2.0, op1=A.mult)
+    tsV(col["u2"], col["r13"], 4.0, A.mult, s2=col["a14"], op1=A.subtract)
+    tsV(col["u1"], col["r13"], 2.0, A.mult, s2=col["u1"], op1=A.add)
+    tsV(col["c7"], c15, -7.0, A.add, s2=col["a14"], op1=A.subtract)
+    ku = tsV(col["r12"], c15, 12.0, A.is_equal)
+    wrows = T.Xn[96:128, :]
+    k_c = copyV(T.c16[0:96, :], T.Xn[0:96, :], landed)
+    copyV(T.Ya[96:128, 13:128:16, :], wrows, k_ya)
+    k_wa = copyV(T.Ya[96:128, 14:128:16, :], wrows)
+    tsV(T.K1[:], T.da[:, 18:146], col["u0"], A.is_equal, ku)
+    k_E = tsV(T.E1[:], T.da[:, 22:150], col["u1"], A.subtract, s2=col["u2"], op1=A.is_equal)
+    kL = mm(b2[:, 0:64], T.c16[0:96, :], T.WJ[0:96, 48:112], True, True, k_c, k_mat)
+    kL1 = copyV(T.L1[:], b2[:, 0:64], kL)
+    tsV(col["j1"], c15, 11.0, A.is_equal, s2=col["r12"], op1=A.subtract)
+    kj = tsV(col["j"], col["r13"], -8.0, A.mult, s2=col["c7"], op1=A.add)
+    lanes(b5, X3, 512, 0, False, k_wa)
+    kp1 = lanes(b4, 0, X3, 0, True)
+    lanes(b7, X3, 512, 1, False)
+    lanes(b3, 0, X3, 1, False)
+
+    k_zr = selG(T.zr[:], T.WJ[:, 0:64], [[0, 64]], A.is_gt, 0.0, 0, 0, k_mat)
     k = selG(T.R[:], T.zr[:, 0:32], [[8, 2], [0, 2], [16, 8]], A.is_gt, 1.0, 0, -1, k_zr)
-    k_wz = selG(T.WT[:], T.WI[:, 0:256], [[0, 256]], A.is_gt, 0.0, 0, 0)
+    for h in range(2):
+        k_wz = selG(T.WT[:, 128 * h:128 * h + 128], I, [[0, 128]], A.is_gt, 0.0, 0, 0)
+    wait("g", ("ld2", 16), inlanes, added)
+    fused(lambda d: T.se[d], T.Xe[:, me, :], "ae")
+    k_w16 = copyG(T.w16[:], T.W0[:, 0:512], 512)
     k_R = selG(T.R[:], T.R[:], [[8, 2], [0, 2], [16, 8]], A.is_ge, 0.0, 7, -1, k)
     for a, b in ((0, 8), (8, 15)):
         for h in range(2):
-            k_e = selG(T.E16[:, h, 16 * a:16 * b], T.Xe[:, 0:b - a, 16 * h:16 * h + 16], [[0, 16 * (b - a)]], A.is_ge, 0.0, 0, 0, ("ae", both))
-    k_wt = selG(T.WT[:, 0:256:16], T.R[:, 0:16], [[0, 16]], A.is_ge, 0.0, 0, 0, k_wz, k_R)
+            k_e = copyG(T.E16[:, h, 16 * a:16 * b], T.Xe[:, 0:b - a, 16 * h:16 * h + 16], 16 * (b - a), ("ae", both))
+    k_wt = copyG(T.WT[:, 0:256:16], T.R[:, 0:16], 16, k_wz, k_R)
+    k_id = done("gi", g.iota(T.win[:, 0:1024], [[1, 1024]], 0, 0, allow_small_or_imprecise_dtypes=True))
 
-    k = copyV(T.c16[0:96, :], T.Xn[0:96, :, :], ("cl", both + 16))
-    kL = mm(T.pR1[:, 0:64], T.c16[0:96, :], T.WI[0:96, 32:96], True, True, k, k_mat)
-    k_a16 = copyS(T.a16[:, VA - 512:512], T.A1[:, VA:1024], ("al", 48))
-    wait("s", ("wl", 32))
-    kk = tsV(T.dr[:], T.db[:, 127:159], 7, A.bitwise_and)
-    k_T = tsV(col["T"], c15, 8.0, A.is_lt)
-    kL1 = copyV(T.L1[:], T.pR1[:, 0:64], kL)
-    kk = tsV(T.OH[:], T.dr[:], 0.0, A.is_equal, kk)
-    wait("v", ("al", 48), ("wl", 32))
+    top, mid, low = slice(512, 1024), slice(X3, 512), slice(1024, 1024 + X3)
+    n2, cx, cm = 512 - X3, X3 // 16, M1 // 16
+    up = ((512, M1), (M1, 1024))
 
-    def relay(out, src, *w):
-        wait("p", *w)
-        for r in range(16):
-            s = -r % 128
-            k = mm(out, T.W7r[:, s:s + 128], src[:, r::16], r == 0, r == 15)
-        return k
+    def lists(src, late, ka, kb, *w):
+        return relay(b2, src, X3, M1, True, True, ka, *w), relay(late, src, M1, 1024 + X3, True, True, *kb)
 
-    pN, pA, pK = (T.pN0, T.pN1), (T.pA0, T.pA1), (T.pK0, T.pK1)
-    H = (slice(0, 512), slice(512, 1024))
-    nA = 1024 - VA
-    kg1v = ttV(T.g1[:, 0:VA], T.W0[:].indirect(T.L1[:, 0:VA // 16]), T.A1[:, 0:VA], A.add, kL1)
-    kg1s = copyS(T.g1[:, VA:1024], T.W0[:].indirect(T.L1[:, VA // 16:64]), kL1)
-    wait("p", k_a16, k_K1, k_B15)
-    mm(T.pA0[:, 0:nA], I, T.a16[:, VA - 512:512], True, False)
-    mm(pN[1][:, W2 - 512:512], T.K1[:], T.a16[:, W2 - 512:512], True, False)
-    mm(pK[1][:, VA - 512:512], T.E1[:], T.a16[:, VA - 512:512], True, False)
-    mm(pA[1][:, VA - 512:VD - 512], T.B15[:], T.a16[:, VA - 512:VD - 512], True, False)
-    ka = mm(T.pA0[:, 0:nA], I, T.g1[:, VA:1024], False, True, kg1s)
-    kr = relay(T.pR0[:, 0:64], T.g1, k_w7r, kg1v)
-    ks1 = copyS(T.W1[:, VA:1024], T.pA0[:, 0:nA], ka)
-    kv1 = copyV(T.W1[:, 0:VA], T.g1[:, 0:VA], kg1v)
-    kl = copyV(T.L2[:], T.pR0[:, 0:64], kr)
-    k_oh = tsV(T.OH[:, 0:1], T.OH[:, 0:1], col["T"], A.mult, kk, k_T)
+    kv = [ttV(T.g1[:, a:b], T.W0[:].indirect(T.L1[:, a // 16:b // 16]), T.A1[:, a - 512:b - 512], A.add, kL1, inlanes, added) for a, b in up]
+    kx = copyS(T.g1[:, mid], T.W0[:].indirect(T.L1[:, cx:32]), kL1, inlanes)
+    ky = copyS(T.g1[:, low], T.W0[:].indirect(T.L1[:, 0:cx]))
+    ka = mm(b5[:, 0:n2], I, T.g1[:, mid], False, True, kx)
+    kr = lists(T.g1, b1, kv[0], (ky, kv[1]), k_w7r, kL1)
+    copyS(T.W1[:, 512:CS], T.g1[:, 512:CS], kv[0])
+    ks1 = copyS(T.W1[:, mid], b5[:, 0:n2], ka)
+    copyV(T.W1[:, CS:M1], T.g1[:, CS:M1], kv[0])
+    copyV(T.W1[:, M1:1024], T.g1[:, M1:1024], kv[1])
+    kv1 = ttV(T.W1[:, 0:X3], T.g1[:, low], b4[:, 0:X3], A.add, ky, kp1)
+    kl = copyV(T.L2[:, cx:cm], b2[:, cx:cm], kr[0])
+    klb = copyS(T.L2[:, cm:64 + cx], b1[:, cm:64 + cx], kr[1])
+    k_E2 = tsV(T.E2[:], T.da[:, 20:148], col["u2"], A.is_equal)
+    kj = tsV(col["j"], col["j"], col["j1"], A.add, kj)
 
-    kn0 = mm(pN[0][:], T.K1[:], T.g1[:, H[0]], True, True)
-    mm(pN[1][:, W2 - 512:512], T.K1[:], T.g1[:, W2:1024], False, False)
-    mm(pK[0][:], T.E1[:], T.g1[:, H[0]], True, False)
-    for a, b in ((512, VA), (VA, 1024)):
-        mm(pK[1][:, a - 512:b - 512], T.E1[:], T.g1[:, a:b], False, False)
-    for a, b in ((512, VA), (VA, VD)):
-        mm(pA[1][:, a - 512:b - 512], T.B15[:], T.g1[:, a:b], False, False)
-    mm(T.pR0[:, 0:W2 - 512], T.K1[:], T.g1[:, 512:W2], True, False, kl)
-    knx = mm(T.pR0[:, VA - 512:W2 - 512], T.K1[:], T.a16[:, VA - 512:W2 - 512], False, True)
-    kg2v = copyV(T.g2[:, 0:V2], T.W1[:].indirect(T.L2[:, 0:V2 // 16]), kl, ks1, kv1)
-    kg2s = copyS(T.g2[:, V2:1024], T.W1[:].indirect(T.L2[:, V2 // 16:64]), kl, ks1, kv1)
-    kn1 = mm(pN[1][:, W2 - 512:512], I, T.g2[:, W2:1024], False, True, kg2s)
-    kr = relay(T.pR1[:, 0:64], T.g2, kL1, kg2v)
-    ttV(T.W2[:, H[0]], T.g2[:, H[0]], pN[0][:], A.add, kn0, kg2v)
-    kw2v = ttV(T.W2[:, 512:W2], T.g2[:, 512:W2], T.pR0[:, 0:W2 - 512], A.add, knx, kg2s)
-    kw2s = copyS(T.W2[:, W2:1024], pN[1][:, W2 - 512:512], kn1)
-    kl4 = copyV(T.L4[:], T.pR1[:, 0:64], kr)
+    mm(b7[:, 0:n2], T.K1[:], T.g1[:, mid], False, False, k_E)
+    kn0 = mm(b6[:], T.K1[:], T.g1[:, top], True, True)
+    knx = mm(b3[:, 0:X3], T.K1[:], T.g1[:, low], False, True)
+    mm(b0[:], T.E1[:], T.g1[:, top], True, False)
+    mm(b5[:, 0:n2], T.E1[:], T.g1[:, mid], True, False, ks1)
+    kv = [copyV(T.g2[:, a:b], T.W1[:].indirect(T.L2[:, a // 16:b // 16]), k, ks1, kv1) for a, b, k in ((512, M1, kl), (M1, V2, klb))]
+    kx = copyS(T.g2[:, mid], T.W1[:].indirect(T.L2[:, cx:32]), kl, ks1, kv1)
+    ky = copyS(T.g2[:, V2:1024 + X3], T.W1[:].indirect(T.L2[:, V2 // 16:64 + cx]), klb)
+    kn1 = mm(b7[:, 0:n2], I, T.g2[:, mid], False, True, kx)
+    kr = lists(T.g2, b4, kv[0], (ky, kv[1]))
+    kw2s = copyS(T.W2[:, mid], b7[:, 0:n2], kn1)
+    for a, b, k in ((512, M1, kv[0]), (M1, V2, kv[1]), (V2, 1024, ky)):
+        ttV(T.W2[:, a:b], T.g2[:, a:b], b6[:, a - 512:b - 512], A.add, kn0, k)
+    kw2v = ttV(T.W2[:, 0:X3], T.g2[:, low], b3[:, 0:X3], A.add, knx)
+    kl4 = copyV(T.L4[:, cx:cm], b2[:, cx:cm], kr[0])
+    klb = copyS(T.L4[:, cm:64 + cx], b4[:, cm:64 + cx], kr[1])
+    km2 = tsV(T.m2[:], T.m1[:, 0:32], col["j"], A.is_lt, k_m0, kj, s2=col["r13"], op1=A.subtract)
+    km1 = tsV(T.OH[:], T.m1[:, 0:32], -7.0, A.add, s2=col["c7"], op1=A.is_equal)
 
-    mm(pK[0][:], T.E2[:], T.g2[:, H[0]], False, False)
-    for o, a, b, k in ((pA[0], 0, X3, ks1), (T.pR1, X3, 512, kl4)):
-        mm(o[:, a:b], T.B15[:], T.g1[:, a:b], True, False, k)
-        mm(o[:, a:b], T.B15[:], T.g2[:, a:b], False, False)
-    ke1 = mm(pK[1][:], T.E2[:], T.g2[:, H[1]], False, True)
-    mm(pA[1][:, 0:VD - 512], T.B15[:], T.g2[:, 512:VD], False, False)
-    kg3v = copyV(T.g3[:, H[1]], T.W2[:].indirect(T.L4[:, 32:64]), kl4, kw2v, kw2s)
-    kx, ky = [copyS(T.g3[:, a:b], T.W2[:].indirect(T.L4[:, a // 16:b // 16]), kl4, kw2v, kw2s) for a, b in ((0, X3), (X3, 512))]
-    ke0 = mm(pK[0][:, 0:X3], I, T.g3[:, 0:X3], False, True, kx)
-    kadx = mm(pA[0][:, 0:X3], T.B15[:], T.g3[:, 0:X3], False, True)
-    kad0 = mm(T.pR1[:, X3:512], T.B15[:], T.g3[:, X3:512], False, True, ky)
-    kr = relay(T.pR0[:, 0:64], T.g3, kg3v, kw2v)
-    kad1 = mm(pA[1][:, 0:VD - 512], T.B15[:], T.g3[:, 512:VD], False, True)
-    kb0 = copyS(T.win[:, 1024:1024 + X3], pK[0][:, 0:X3], ke0)
-    ttV(T.win[:, 1536:2048], T.g3[:, H[1]], pK[1][:], A.add, ke1, kg3v)
-    kb1 = ttV(T.win[:, 1024 + X3:1536], T.g3[:, X3:512], pK[0][:, X3:512], A.add, kb0, ky)
-    kad = [copyS(T.adF[:, 0:X3], pA[0][:, 0:X3], kadx)]
-    copyS(T.adF[:, X3:512], T.pR1[:, X3:512], kad0)
-    kad.append(copyS(T.adF[:, 512:VC], pA[1][:, 0:VC - 512], kad1))
-    kl8 = copyV(T.L8[:], T.pR0[:, 0:64], kr)
+    mm(b5[:, 0:n2], T.E2[:], T.g2[:, mid], False, False, k_E2)
+    mm(b5[:, 0:n2], T.D13[:], T.w16[:, mid], False, False, k_w16, k_d13)
+    ke0 = mm(b0[:], T.E2[:], T.g2[:, top], False, True)
+    mm(b1[:, 0:X3], T.D13[:], T.w16[:, 0:X3], True, False)
+    mm(b1[:, 0:X3], T.E1[:], T.g1[:, low], False, False)
+    mm(b1[:, 0:X3], T.E2[:], T.g2[:, low], False, True)
+    kv = [copyV(T.g3[:, a:b], T.W2[:].indirect(T.L4[:, a // 16:b // 16]), k, kw2v, kw2s) for (a, b), k in zip(up, (kl4, klb))]
+    kx = copyS(T.g3[:, mid], T.W2[:].indirect(T.L4[:, cx:32]), kl4, kw2v, kw2s)
+    ky = copyS(T.g3[:, 0:X3], T.W2[:].indirect(T.L4[:, 64:64 + cx]), klb)
+    ke1 = mm(b5[:, 0:n2], I, T.g3[:, mid], False, True, kx)
+    relay(b2, T.g3, X3, M1, True, False, kl4, kv[0])
+    relay(b2, T.g3, M1, 1024, False, False, kv[1])
+    kr = relay(b2, T.g3, 0, X3, False, True, ky)
+    kb0 = copyS(T.win[:, 1024 + X3:1536], b5[:, 0:n2], ke1)
+    kb1 = [ttV(T.win[:, 1024 + a:1024 + b], T.g3[:, a:b], b0[:, a - 512:b - 512], A.add, ke0, k) for (a, b), k in zip(up, kv)]
+    kb2 = ttV(T.win[:, 1024:1024 + X3], T.g3[:, 0:X3], b1[:, 0:X3], A.add, ky, ke1)
+    copyS(T.ad[:, VC:512], b5[:, VC - X3:n2], scale=col["r13"])
+    kad = {1024: tsV(T.ad[:, M1:1024], T.win[:, 1024 + M1:2048], col["r13"], A.mult, kb1[1]),
+           M1: copyS(T.ad[:, 512:M1], T.win[:, 1536:1024 + M1], kb1[0], scale=col["r13"])}
+    kl8 = copyV(T.L8[:], b2[:, 0:64], kr)
+    k_oh = ttV(T.OH[:], T.OH[:], T.m2[:], A.subtract, km1, km2)
 
     kmask = {}
+    todo = list(MS)
 
-    def mask(t, a, b, k):
-        k = copyS(T.mk[:, 512 * t + 128 * a:512 * t + 128 * b], T.OH[:].indirect(T.lu[:, 32 * t + 8 * a:32 * t + 8 * b]), k, k_oh)
+    def mask(copy=copyS):
+        a, b = todo.pop(0)
+        k = copy(T.mk[:, 64 * a:64 * b], T.OH[:].indirect(T.lu[:, 4 * a:4 * b]), klu, k_oh)
         for i in range(a, b):
-            kmask[t, i] = k
+            kmask[i] = k
+
+    def eight(bank, a, b, stop, *w):
+        mm(bank[:, 0:b - a], T.D13[:], T.w16[:, a:b], True, False, *w)
+        for x in (T.g1, T.g2):
+            if b > X3:
+                mm(bank[:, X3 - a:b - a], T.D13[:], x[:, X3:b], False, False)
+            mm(bank[:, 0:min(b, X3) - a], T.D13[:], x[:, 1024 + a:1024 + min(b, X3)], False, False)
+        return mm(bank[:, 0:b - a], T.D13[:], T.g3[:, a:b], False, stop)
 
     free = {2: kw2v, 3: kw2s}
-    kprev = [kb0, kb1]
+    kprev = [kb0, kb2]
     for B in range(2, 5):
-        a, u = 1024 * (B - 1), VD
-        src = T.win[:, a:a + 1024]
-        bank = pN[B % 2][:, 0:1024 - u]
-        cuts = (0, X3, VC) if B == 2 else (0, VC)
-        for u0, u1 in zip(cuts, cuts[1:]):
-            ttV(T.win[:, a + 1024 + u0:a + 1024 + u1], src.indirect(T.L8[:, u0 // 16:u1 // 16]), T.adF[:, u0:u1], A.add, kl8, kad[0] if u1 == X3 else kad[1], *kprev)
-        kg = copyS(T.gb[:, u:1024], src.indirect(T.L8[:, u // 16:64]), kl8, *kprev)
-        kg2 = copyS(T.gb[:, VC:u], src.indirect(T.L8[:, VC // 16:u // 16]))
-        kv = ttV(T.win[:, a + 1024 + VC:a + 1024 + u], T.gb[:, VC:u], pA[1][:, VC - 512:u - 512], A.add, kg2)
-        mm(bank, T.B15[:], T.a16[:, u - 512:512], True, False, free[B])
-        for x in (T.g1, T.g2, T.g3):
-            mm(bank, T.B15[:], x[:, u:1024], False, False)
+        a = 1024 * B
+        src = T.win[:, a - 1024:a]
+        pb = (b6, b7)[B % 2]
+        bank = pb[:, 0:VD]
+        eight(pb, 0, VD, False, free[B])
         if B == 2:
-            wait("p", k_e, kb1)
+            kadp = eight(b4, VD, VC, True, klb)
+        for u0, u1 in ((M1, 1024), (VC, M1)) if B == 2 else ((VC, 1024),):
+            ttV(T.win[:, a + u0:a + u1], src.indirect(T.L8[:, u0 // 16:u1 // 16]), T.ad[:, u0:u1], A.add, kl8, kad[u1], *kprev)
+        kg = copyS(T.gb[:, 0:VD], src.indirect(T.L8[:, 0:VD // 16]), kl8, *kprev)
+        kg2 = copyS(T.gb[:, VD:VC], src.indirect(T.L8[:, VD // 16:VC // 16]))
+        kv = ttV(T.win[:, a + VD:a + VC], T.gb[:, VD:VC], b4[:, 0:VC - VD], A.add, kg2, kadp)
+        if B == 2:
+            wait("p", k_e, kw2v)
             for t in range(8):
                 s = 16 * ((N - t) % N)
                 for h in range(2):
-                    kt = mm(pK[0][:, 32 * t + h:32 * t + 32:2], T.E16[:, h, s:s + 128], T.WI[:, t:128:8], t + h == 0, t + h == 8)
-            k_h = copyS(T.h16[:, 0:64], pK[0][:, 0:64], kt, scale=0.125, bias=1024.4375)
-        km = mm(bank, I, T.gb[:, u:1024], False, True, kg)
+                    kt = mm(b3[:, 32 * t + h:32 * t + 32:2], T.E16[:, h, s:s + 128], T.WJ[:, 16 + t:144:8], t + h == 0, t + h == 8)
+            k_h = copyS(T.h16[:, 0:64], b3[:, 0:64], kt, scale=0.125, bias=1024.4375)
+        km = mm(bank, I, T.gb[:, 0:VD], False, True, kg)
         if B > 2:
-            mask(0, 2 * B - 6, 2 * B - 5, klu)
-        ks = copyS(T.win[:, a + 1024 + u:a + 2048], bank, km)
+            mask()
+        ks = copyS(T.win[:, a:a + VD], bank, km)
         free[B + 2] = ks
         kprev = [kv, ks]
         if B == 2:
-            klu = copyV(T.lu[:], pK[0][:, 0:256], k_h)
-            mm(pK[1][:, 0:32], T.c16[0:96, :], T.WI[0:96, 0:32], True, False)
-            ko = mm(pK[1][:, 0:32], T.WH[:], T.h16[:, 0:32], False, True, k_h, k_wh)
+            klu = copyV(T.lu[:], b3[:, 0:256], k_h)
+            mm(b5[:, 0:32], T.c16[0:96, :], T.WJ[0:96, 16:48], True, False, kad[M1])
+            ko = mm(b5[:, 0:32], T.WH[:], T.h16[:, 0:32], False, True, k_h, k_wh)
         if B == 3:
-            koff0 = tsV(T.off[:], pK[1][:, 0:32], -2.0 ** 20, A.add, ko)
+            mask()
+            koff0 = tsV(T.off[:], b5[:, 0:32], -2.0 ** 20, A.add, ko)
+            k7 = ks
+        if B > 2:
+            mask(copyV)
 
     krel = {}
     koff = [koff0] * 4
-    F = T.pA0
+    F = b5
     Gs = (T.G0, T.G1)
-    banks = (T.pR0, T.pR1, T.pN1, T.pK1)
-
-    def direct(t, z, kinds, last=False):
-        for u in range(8):
-            for kind in kinds:
-                a = 64 * kind + 32 * z
-                k = mm(F[a:a + 32, u:64:8], Gs[t % 2][:, 256 * z + u:256 * z + 256:8], T.R[:, 16 * kind + t:16 * kind + t + 8], False, last and u == 7)
-        return k
+    banks = (b0, b1, b2, b7)
 
     def gather(t, i):
         G, a = Gs[t % 2], 128 * i
         k = ttV(G[:, a:a + 128], T.win[:].indirect(T.off[:, 8 * i:8 * i + 8]), T.mk[:, 512 * t + a:512 * t + a + 128], A.mult,
-                kmask[t, i], koff[i], k_id, *kprev)
+                kmask[8 * t + 2 * i], kmask[8 * t + 2 * i + 1], koff[i], k_id, *kprev)
         if t < 7:
             o = banks[i][:, 0:8]
             c = 32 * (t + 1) + 8 * i
             mm(o, T.WH[:], T.h16[:, c:c + 8], True, False, koff[i], *([k_h2] if t else []))
             for r in range(16):
                 krel[i] = mm(o, T.WT[:, 112 - r:240 - r], G[:, a + r:a + 128:16], False, r == 15, k)
-        if i % 2:
+        if i == 3:
             wait("p", k)
-            return direct(t, i // 2, (0, 1) if t == 7 else (1,), last=t == 7)
+            for u in range(8):
+                for kind in (0, 1) if t == 7 else (1,):
+                    k = mm(F[64 * kind:64 * kind + 64, u:64:8], G[:, u:512:8], T.R[:, 16 * kind + t:16 * kind + t + 8], False, t == 7 and u == 7)
+            return k
 
-    def offsets(i):
-        koff[i] = tsV(T.off[:, 8 * i:8 * i + 8], banks[i][:, 0:8], -2.0 ** 20, A.add, krel[i])
+    def offsets(t, i):
+        if 4 * t + i >= LATE:
+            koff[i] = copyS(T.off[:, 8 * i:8 * i + 8], banks[i][:, 0:8], krel[i], bias=-2.0 ** 20)
+        else:
+            koff[i] = tsV(T.off[:, 8 * i:8 * i + 8], banks[i][:, 0:8], -2.0 ** 20, A.add, krel[i])
 
-    mask(0, 1, 2, klu)
-    mask(0, 3, 4, klu)
-    mask(1, 0, 2, klu)
-    k_h2 = copyS(T.h16[:, 64:256], pK[0][:, 64:256], scale=0.125, bias=1024.4375)
-    mask(1, 2, 4, klu)
-    mask(2, 0, 2, klu)
-    mask(2, 2, 4, klu)
-    for t in range(3, 8):
-        mask(t, 0, 4, klu)
-    wait("p", k_wt, kl8, kad[1], klu, k_zr)
+    while todo:
+        if todo[0][0] == 12:
+            k_h2 = copyS(T.h16[:, 64:256], b3[:, 64:256], scale=0.125, bias=1024.4375)
+        mask()
+    wait("p", k_wt, kl8, kb2, k7, koff0, k_zr)
     mm(F[:, 0:64], I, T.zr[:], True, False)
     for i in range(3):
         gather(0, i)
     for t in range(1, 8):
-        if t not in EVEN:
-            gather(t - 1, 3)
-        offsets(0)
-        if t in EVEN:
-            gather(t - 1, 3)
-        for i in range(3):
-            offsets(i + 1)
-            gather(t, i)
+        for i in range(4):
+            offsets(t, i)
+            gather(t - (i == 0), (i - 1) % 4)
     kf = gather(7, 3)
     kO = copyV(T.O[:], F[:, 0:64], kf)
 
     wait("g", kO)
-    fused(lambda d: T.O[:, 8 * d:8 * d + 8], T.ri[me], "ar", (0, 1))
+    fused(lambda d: T.O[:, 8 * d:8 * d + 8], T.ri[me], "ar")
     wait("y", kO)
     Y.dma_start(out=T.ri[me], in_=T.O[:, 8 * me:8 * me + 8]).then_inc(sem.ar, 16)
     for e in (Y, S):

from concourse.bass import DstId, RemoteDMATransfer
from concourse.mybir import AluOpType, ActivationFunctionType

X3 = 224
M1 = 864
CS = 640
V2 = 960
VC = 384
VD = 160
LATE = 24
MS = ((0, 2), (2, 4), (6, 7), (4, 6), (7, 8), (8, 12), (12, 16), (16, 22), (22, 30), (30, 40), (40, 52), (52, 64))
SCRATCH = {"OH": ("sbuf", [128, 32], "float32"), "mk": ("sbuf", [128, 4096], "bfloat16"), "Xe": ("sbuf", [128, 8, 32], "int32"),
           "E16": ("sbuf", [128, 2, 240], "float16"), "Ya": ("sbuf", [128, 130, 16], "bfloat16"),
           "ri": ("dram", [8, 128, 8], "float32"), "sm": ("dram", [8, 160, 16], "int32"), "se": ("dram", [8, 128, 32], "int32"),
           "rm": ("dram", [8, 128, 16], "int32")}
for _d, _l in (("int32", "W0:1024 A1:512 Xn:128 pc:1 ci:8 da:160 idv:64"),
               ("float32", "win:5120 W1:1024 W2:1024 O:64 cf:24 m1:40 m2:32"),
               ("float16", "g1:1344 g2:1344 g3:1024 w16:512 ad:1024 gb:512 c16:128 h16:256 G0:512 G1:512 K1:128 E1:128 E2:128 D13:128 WJ:160 WH:128 W7r:144 WT:256 R:32 zr:64"),
               ("uint16", "L1:64 L2:96 L4:96 L8:64 lu:256 off:32")):
    for _e in _l.split():
        SCRATCH[_e.split(":")[0]] = ("sbuf", [128, int(_e.split(":")[1])], _d)
for _n in range(8):
    SCRATCH["b%d" % _n] = ("psum", [128, 512], "float32")
SEMAPHORES = ["ld", "ld2", "ld3", "own", "am", "cl", "wl", "al", "ae", "v", "s", "p", "gi", "ls", "ar", "fin"]


def rank_program(g, core, T, topo):
    me = T.rank_of(core)
    if me is None:
        return
    V, S, P, Y = g.vector, g.scalar, g.tensor, g.sync
    A = AluOpType
    COPY = ActivationFunctionType.Copy
    N = len(T.cores)
    others = [(me + d) % N for d in range(1, N)]
    sem = T.sem
    cnt = {"v": 0, "s": 0, "p": 0, "gi": 0}
    seen = {}
    queues = {"v": V, "s": S, "p": P, "g": g, "y": Y}
    b0, b1, b2, b3, b4, b5, b6, b7 = [T["b%d" % n] for n in range(8)]

    def wait(q, *toks):
        for name, n in toks:
            if n > seen.get((q, name), 0):
                queues[q].wait_ge(sem[name], n)
                seen[(q, name)] = n

    def done(name, ins):
        cnt[name] += 1
        ins.then_inc(sem[name], 1)
        return (name, cnt[name])

    def copyV(out, in_, *w):
        wait("v", *w)
        return done("v", V.tensor_copy(out=out, in_=in_))

    def tsV(out, in0, s1, op0, *w, s2=None, op1=None):
        wait("v", *w)
        if op1 is None:
            return done("v", V.tensor_scalar(out=out, in0=in0, scalar1=s1, scalar2=None, op0=op0))
        return done("v", V.tensor_scalar(out=out, in0=in0, scalar1=s1, scalar2=s2, op0=op0, op1=op1))

    def ttV(out, in0, in1, op, *w):
        wait("v", *w)
        return done("v", V.tensor_tensor(out=out, in0=in0, in1=in1, op=op))

    def copyS(out, in_, *w, scale=1.0, bias=0.0):
        wait("s", *w)
        return done("s", S.activation(out=out, in_=in_, func=COPY, bias=bias, scale=scale))

    def selG(out, in_, pattern, op, fill, base, cm, *w):
        wait("g", *w)
        return done("gi", g.affine_select(out, in_, pattern, op, fill, base, cm))

    def copyG(out, in_, n, *w):
        return selG(out, in_, [[0, n]], A.is_ge, 0.0, 0, 0, *w)

    def mm(out, lhsT, rhs, start, stop, *w):
        wait("p", *w)
        ins = P.matmul(out=out, lhsT=lhsT, rhs=rhs, start=start, stop=stop)
        return done("p", ins) if stop else None

    def fused(src, dst, rsem, ks=(0, 1)):
        tr = []
        for n, d in enumerate(others):
            c = T.cores[d]
            rid, pid, _ = topo.addr(c)
            eng = topo.engines(core, c)
            m = sum(1 << eng[(2 * n + j) % len(eng)] for j in ks)
            tr.append(RemoteDMATransfer(src=src(d), dst=dst, dst_ids=[DstId(rid=rid, pnc=pid)], dma_engine_mask=m, remote_sem=sem[rsem]))
        g.remote_dma_fused(tr, local_sem=sem.ls)

    mine = slice(16 * me, 16 * me + 16)
    both = 16 + 2 * (N - 1)
    for q, out, in_, name in ((Y, T.sm[:, 32:96, :], T.nx[:, :], "ld"), (S, T.sm[:, 96:160, :], T.w[:, :], "ld"),
                              (Y, T.sm[:, 0:32, :], T.x[:, :], "ld3"), (S, T.rm[me, 64:128, :], T.w[me, :], "own"),
                              (Y, T.rm[me, 0:64, :], T.nx[me, :], "own"), (S, T.Xn[0:32, mine], T.x[mine, :], "cl"),
                              (Y, T.Xn[32:96, mine], T.nx[me, :], "cl"), (Y, T.Xn[96:128, mine], T.w[me, 0:512], "cl")):
        q.dma_start(out=out, in_=in_).then_inc(sem[name], 16)
    landed = ("cl", both + 32)

    k_idv = done("gi", g.iota(T.idv[:], [[1, 64]], 0, 64))
    k_pc = done("gi", g.iota(T.pc[:, 0:1], [[0, 1]], 0, 1))
    k_da = done("gi", g.iota(T.da[:], [[1, 160]], -16, -1))
    g.wait_ge(sem.ld, 32)
    fused(lambda d: T.sm[d, 32:160, :], T.rm[me], "am", (0,))
    g.wait_ge(sem.ld3, 16)
    fused(lambda d: T.sm[d, 0:128, :], T.Xn[:, mine], "cl")
    g.iota(T.m1[:, 0:1], [[0, 1]], 6, 0, allow_small_or_imprecise_dtypes=True)
    k_m0 = done("gi", g.iota(T.m1[:, 1:33], [[0, 4], [1, 8]], 0, 0, allow_small_or_imprecise_dtypes=True))

    names = ["r7", "r12", "r13", "r15", "a14", "c7", "j", "j1", "u0", "u1", "u2"]
    col = {n: T.cf[:, i:i + 1] for i, n in enumerate(names)}
    c15 = T.ci[:, 0:1]
    k_z = done("v", V.memset(T.Ya[:, 0:65, :], 0.0))
    k_ya = copyS(T.Ya[:, 65:130, :], T.Ya[:, 0:65, :], k_z)
    k_idl = tsV(T.idv[:], T.idv[:], 1023, A.bitwise_and, k_idv)
    k_w0 = done("v", V.memset(T.W0[:], 0))
    kc = tsV(c15, T.pc[:, 0:1], 15, A.bitwise_and, k_pc)
    wait("y", k_w0, k_idl)
    Y.dma_start(out=T.W0[6::16, :], in_=T.idv[:]).then_inc(sem.wl, 16)
    Y.dma_start(out=T.se[:], in_=T.e[:, :]).then_inc(sem.ld2, 16)
    Y.dma_start(out=T.Xe[:, me, :], in_=T.e[mine, :]).then_inc(sem.ae, 16)
    k_a1 = done("v", V.memset(T.A1[:], 0))
    tsV(col["r7"], c15, 7.0, A.is_equal, kc)
    tsV(col["r13"], c15, 13.0, A.is_equal)
    tsV(col["r15"], c15, 15.0, A.is_equal)
    tsV(col["a14"], c15, 14.0, A.is_ge)
    tsV(col["u1"], c15, 14.0, A.is_equal, s2=201.0, op1=A.mult)
    k_mat = tsV(T.WJ[:], T.da[:], 0.0, A.is_equal, k_da)
    I = T.WJ[:, 16:144]

    for e in (Y, S):
        e.wait_ge(sem.own, 32)
        e.wait_ge(sem.am, N - 1)
    wait("y", k_a1)
    wait("s", k_a1)
    wtop = T.rm[:, 96:128, :]
    Y.dma_start(out=T.W0[7::8, :], in_=T.rm[:]).then_inc(sem.wl, 16)
    S.dma_start(out=T.W0[13::16, :], in_=T.rm[:, 64:128, :]).then_inc(sem.wl, 16)
    Y.dma_start(out=T.A1[13::16, :], in_=wtop).then_inc(sem.al, 16)
    S.dma_start(out=T.A1[14::16, :], in_=wtop).then_inc(sem.al, 16)
    inlanes, added = ("wl", 48), ("al", 32)
    k_w7r = copyS(T.W7r[:], T.WJ[:, 8:152], k_mat, scale=col["r7"])
    k_d13 = copyS(T.D13[:], I, scale=col["r13"])
    k_wh = copyS(T.WH[:], I, scale=1024.0)

    def lanes(bank, a, b, s, stop, *w):
        wait("p", *w)
        for r in range(16):
            k = mm(bank[:, r:b - a:16], T.Ya[96:128, s:s + 128, r], T.WJ[96:128, 112 + a // 16:112 + b // 16], r == 0, stop and r == 15)
        return k

    def relay(bank, src, a, b, start, stop, *w):
        wait("p", *w)
        for r in range(16):
            k = mm(bank[:, a // 16:b // 16], T.W7r[:, 15 - r:143 - r], src[:, a + r:b:16], start and r == 0, stop and r == 15)
        return k

    tsV(col["u0"], col["r13"], col["r15"], A.subtract, k_mat, s2=2.0, op1=A.mult)
    tsV(col["u2"], col["r13"], 4.0, A.mult, s2=col["a14"], op1=A.subtract)
    tsV(col["u1"], col["r13"], 2.0, A.mult, s2=col["u1"], op1=A.add)
    tsV(col["c7"], c15, -7.0, A.add, s2=col["a14"], op1=A.subtract)
    ku = tsV(col["r12"], c15, 12.0, A.is_equal)
    wrows = T.Xn[96:128, :]
    k_c = copyV(T.c16[0:96, :], T.Xn[0:96, :], landed)
    copyV(T.Ya[96:128, 13:128:16, :], wrows, k_ya)
    k_wa = copyV(T.Ya[96:128, 14:128:16, :], wrows)
    tsV(T.K1[:], T.da[:, 18:146], col["u0"], A.is_equal, ku)
    k_E = tsV(T.E1[:], T.da[:, 22:150], col["u1"], A.subtract, s2=col["u2"], op1=A.is_equal)
    kL = mm(b2[:, 0:64], T.c16[0:96, :], T.WJ[0:96, 48:112], True, True, k_c, k_mat)
    kL1 = copyV(T.L1[:], b2[:, 0:64], kL)
    tsV(col["j1"], c15, 11.0, A.is_equal, s2=col["r12"], op1=A.subtract)
    kj = tsV(col["j"], col["r13"], -8.0, A.mult, s2=col["c7"], op1=A.add)
    lanes(b5, X3, 512, 0, False, k_wa)
    kp1 = lanes(b4, 0, X3, 0, True)
    lanes(b7, X3, 512, 1, False)
    lanes(b3, 0, X3, 1, False)

    k_zr = selG(T.zr[:], T.WJ[:, 0:64], [[0, 64]], A.is_gt, 0.0, 0, 0, k_mat)
    k = selG(T.R[:], T.zr[:, 0:32], [[8, 2], [0, 2], [16, 8]], A.is_gt, 1.0, 0, -1, k_zr)
    for h in range(2):
        k_wz = selG(T.WT[:, 128 * h:128 * h + 128], I, [[0, 128]], A.is_gt, 0.0, 0, 0)
    wait("g", ("ld2", 16), inlanes, added)
    fused(lambda d: T.se[d], T.Xe[:, me, :], "ae")
    k_w16 = copyG(T.w16[:], T.W0[:, 0:512], 512)
    k_R = selG(T.R[:], T.R[:], [[8, 2], [0, 2], [16, 8]], A.is_ge, 0.0, 7, -1, k)
    for a, b in ((0, 8), (8, 15)):
        for h in range(2):
            k_e = copyG(T.E16[:, h, 16 * a:16 * b], T.Xe[:, 0:b - a, 16 * h:16 * h + 16], 16 * (b - a), ("ae", both))
    k_wt = copyG(T.WT[:, 0:256:16], T.R[:, 0:16], 16, k_wz, k_R)
    k_id = done("gi", g.iota(T.win[:, 0:1024], [[1, 1024]], 0, 0, allow_small_or_imprecise_dtypes=True))

    top, mid, low = slice(512, 1024), slice(X3, 512), slice(1024, 1024 + X3)
    n2, cx, cm = 512 - X3, X3 // 16, M1 // 16
    up = ((512, M1), (M1, 1024))

    def lists(src, late, ka, kb, *w):
        return relay(b2, src, X3, M1, True, True, ka, *w), relay(late, src, M1, 1024 + X3, True, True, *kb)

    kv = [ttV(T.g1[:, a:b], T.W0[:].indirect(T.L1[:, a // 16:b // 16]), T.A1[:, a - 512:b - 512], A.add, kL1, inlanes, added) for a, b in up]
    kx = copyS(T.g1[:, mid], T.W0[:].indirect(T.L1[:, cx:32]), kL1, inlanes)
    ky = copyS(T.g1[:, low], T.W0[:].indirect(T.L1[:, 0:cx]))
    ka = mm(b5[:, 0:n2], I, T.g1[:, mid], False, True, kx)
    kr = lists(T.g1, b1, kv[0], (ky, kv[1]), k_w7r, kL1)
    copyS(T.W1[:, 512:CS], T.g1[:, 512:CS], kv[0])
    ks1 = copyS(T.W1[:, mid], b5[:, 0:n2], ka)
    copyV(T.W1[:, CS:M1], T.g1[:, CS:M1], kv[0])
    copyV(T.W1[:, M1:1024], T.g1[:, M1:1024], kv[1])
    kv1 = ttV(T.W1[:, 0:X3], T.g1[:, low], b4[:, 0:X3], A.add, ky, kp1)
    kl = copyV(T.L2[:, cx:cm], b2[:, cx:cm], kr[0])
    klb = copyS(T.L2[:, cm:64 + cx], b1[:, cm:64 + cx], kr[1])
    k_E2 = tsV(T.E2[:], T.da[:, 20:148], col["u2"], A.is_equal)
    kj = tsV(col["j"], col["j"], col["j1"], A.add, kj)

    mm(b7[:, 0:n2], T.K1[:], T.g1[:, mid], False, False, k_E)
    kn0 = mm(b6[:], T.K1[:], T.g1[:, top], True, True)
    knx = mm(b3[:, 0:X3], T.K1[:], T.g1[:, low], False, True)
    mm(b0[:], T.E1[:], T.g1[:, top], True, False)
    mm(b5[:, 0:n2], T.E1[:], T.g1[:, mid], True, False, ks1)
    kv = [copyV(T.g2[:, a:b], T.W1[:].indirect(T.L2[:, a // 16:b // 16]), k, ks1, kv1) for a, b, k in ((512, M1, kl), (M1, V2, klb))]
    kx = copyS(T.g2[:, mid], T.W1[:].indirect(T.L2[:, cx:32]), kl, ks1, kv1)
    ky = copyS(T.g2[:, V2:1024 + X3], T.W1[:].indirect(T.L2[:, V2 // 16:64 + cx]), klb)
    kn1 = mm(b7[:, 0:n2], I, T.g2[:, mid], False, True, kx)
    kr = lists(T.g2, b4, kv[0], (ky, kv[1]))
    kw2s = copyS(T.W2[:, mid], b7[:, 0:n2], kn1)
    for a, b, k in ((512, M1, kv[0]), (M1, V2, kv[1]), (V2, 1024, ky)):
        ttV(T.W2[:, a:b], T.g2[:, a:b], b6[:, a - 512:b - 512], A.add, kn0, k)
    kw2v = ttV(T.W2[:, 0:X3], T.g2[:, low], b3[:, 0:X3], A.add, knx)
    kl4 = copyV(T.L4[:, cx:cm], b2[:, cx:cm], kr[0])
    klb = copyS(T.L4[:, cm:64 + cx], b4[:, cm:64 + cx], kr[1])
    km2 = tsV(T.m2[:], T.m1[:, 0:32], col["j"], A.is_lt, k_m0, kj, s2=col["r13"], op1=A.subtract)
    km1 = tsV(T.OH[:], T.m1[:, 0:32], -7.0, A.add, s2=col["c7"], op1=A.is_equal)

    mm(b5[:, 0:n2], T.E2[:], T.g2[:, mid], False, False, k_E2)
    mm(b5[:, 0:n2], T.D13[:], T.w16[:, mid], False, False, k_w16, k_d13)
    ke0 = mm(b0[:], T.E2[:], T.g2[:, top], False, True)
    mm(b1[:, 0:X3], T.D13[:], T.w16[:, 0:X3], True, False)
    mm(b1[:, 0:X3], T.E1[:], T.g1[:, low], False, False)
    mm(b1[:, 0:X3], T.E2[:], T.g2[:, low], False, True)
    kv = [copyV(T.g3[:, a:b], T.W2[:].indirect(T.L4[:, a // 16:b // 16]), k, kw2v, kw2s) for (a, b), k in zip(up, (kl4, klb))]
    kx = copyS(T.g3[:, mid], T.W2[:].indirect(T.L4[:, cx:32]), kl4, kw2v, kw2s)
    ky = copyS(T.g3[:, 0:X3], T.W2[:].indirect(T.L4[:, 64:64 + cx]), klb)
    ke1 = mm(b5[:, 0:n2], I, T.g3[:, mid], False, True, kx)
    relay(b2, T.g3, X3, M1, True, False, kl4, kv[0])
    relay(b2, T.g3, M1, 1024, False, False, kv[1])
    kr = relay(b2, T.g3, 0, X3, False, True, ky)
    kb0 = copyS(T.win[:, 1024 + X3:1536], b5[:, 0:n2], ke1)
    kb1 = [ttV(T.win[:, 1024 + a:1024 + b], T.g3[:, a:b], b0[:, a - 512:b - 512], A.add, ke0, k) for (a, b), k in zip(up, kv)]
    kb2 = ttV(T.win[:, 1024:1024 + X3], T.g3[:, 0:X3], b1[:, 0:X3], A.add, ky, ke1)
    copyS(T.ad[:, VC:512], b5[:, VC - X3:n2], scale=col["r13"])
    kad = {1024: tsV(T.ad[:, M1:1024], T.win[:, 1024 + M1:2048], col["r13"], A.mult, kb1[1]),
           M1: copyS(T.ad[:, 512:M1], T.win[:, 1536:1024 + M1], kb1[0], scale=col["r13"])}
    kl8 = copyV(T.L8[:], b2[:, 0:64], kr)
    k_oh = ttV(T.OH[:], T.OH[:], T.m2[:], A.subtract, km1, km2)

    kmask = {}
    todo = list(MS)

    def mask(copy=copyS):
        a, b = todo.pop(0)
        k = copy(T.mk[:, 64 * a:64 * b], T.OH[:].indirect(T.lu[:, 4 * a:4 * b]), klu, k_oh)
        for i in range(a, b):
            kmask[i] = k

    def eight(bank, a, b, stop, *w):
        mm(bank[:, 0:b - a], T.D13[:], T.w16[:, a:b], True, False, *w)
        for x in (T.g1, T.g2):
            if b > X3:
                mm(bank[:, X3 - a:b - a], T.D13[:], x[:, X3:b], False, False)
            mm(bank[:, 0:min(b, X3) - a], T.D13[:], x[:, 1024 + a:1024 + min(b, X3)], False, False)
        return mm(bank[:, 0:b - a], T.D13[:], T.g3[:, a:b], False, stop)

    free = {2: kw2v, 3: kw2s}
    kprev = [kb0, kb2]
    for B in range(2, 5):
        a = 1024 * B
        src = T.win[:, a - 1024:a]
        pb = (b6, b7)[B % 2]
        bank = pb[:, 0:VD]
        eight(pb, 0, VD, False, free[B])
        if B == 2:
            kadp = eight(b4, VD, VC, True, klb)
        for u0, u1 in ((M1, 1024), (VC, M1)) if B == 2 else ((VC, 1024),):
            ttV(T.win[:, a + u0:a + u1], src.indirect(T.L8[:, u0 // 16:u1 // 16]), T.ad[:, u0:u1], A.add, kl8, kad[u1], *kprev)
        kg = copyS(T.gb[:, 0:VD], src.indirect(T.L8[:, 0:VD // 16]), kl8, *kprev)
        kg2 = copyS(T.gb[:, VD:VC], src.indirect(T.L8[:, VD // 16:VC // 16]))
        kv = ttV(T.win[:, a + VD:a + VC], T.gb[:, VD:VC], b4[:, 0:VC - VD], A.add, kg2, kadp)
        if B == 2:
            wait("p", k_e, kw2v)
            for t in range(8):
                s = 16 * ((N - t) % N)
                for h in range(2):
                    kt = mm(b3[:, 32 * t + h:32 * t + 32:2], T.E16[:, h, s:s + 128], T.WJ[:, 16 + t:144:8], t + h == 0, t + h == 8)
            k_h = copyS(T.h16[:, 0:64], b3[:, 0:64], kt, scale=0.125, bias=1024.4375)
        km = mm(bank, I, T.gb[:, 0:VD], False, True, kg)
        if B > 2:
            mask()
        ks = copyS(T.win[:, a:a + VD], bank, km)
        free[B + 2] = ks
        kprev = [kv, ks]
        if B == 2:
            klu = copyV(T.lu[:], b3[:, 0:256], k_h)
            mm(b5[:, 0:32], T.c16[0:96, :], T.WJ[0:96, 16:48], True, False, kad[M1])
            ko = mm(b5[:, 0:32], T.WH[:], T.h16[:, 0:32], False, True, k_h, k_wh)
        if B == 3:
            mask()
            koff0 = tsV(T.off[:], b5[:, 0:32], -2.0 ** 20, A.add, ko)
            k7 = ks
        if B > 2:
            mask(copyV)

    krel = {}
    koff = [koff0] * 4
    F = b5
    Gs = (T.G0, T.G1)
    banks = (b0, b1, b2, b7)

    def gather(t, i):
        G, a = Gs[t % 2], 128 * i
        k = ttV(G[:, a:a + 128], T.win[:].indirect(T.off[:, 8 * i:8 * i + 8]), T.mk[:, 512 * t + a:512 * t + a + 128], A.mult,
                kmask[8 * t + 2 * i], kmask[8 * t + 2 * i + 1], koff[i], k_id, *kprev)
        if t < 7:
            o = banks[i][:, 0:8]
            c = 32 * (t + 1) + 8 * i
            mm(o, T.WH[:], T.h16[:, c:c + 8], True, False, koff[i], *([k_h2] if t else []))
            for r in range(16):
                krel[i] = mm(o, T.WT[:, 112 - r:240 - r], G[:, a + r:a + 128:16], False, r == 15, k)
        if i == 3:
            wait("p", k)
            for u in range(8):
                for kind in (0, 1) if t == 7 else (1,):
                    k = mm(F[64 * kind:64 * kind + 64, u:64:8], G[:, u:512:8], T.R[:, 16 * kind + t:16 * kind + t + 8], False, t == 7 and u == 7)
            return k

    def offsets(t, i):
        if 4 * t + i >= LATE:
            koff[i] = copyS(T.off[:, 8 * i:8 * i + 8], banks[i][:, 0:8], krel[i], bias=-2.0 ** 20)
        else:
            koff[i] = tsV(T.off[:, 8 * i:8 * i + 8], banks[i][:, 0:8], -2.0 ** 20, A.add, krel[i])

    while todo:
        if todo[0][0] == 12:
            k_h2 = copyS(T.h16[:, 64:256], b3[:, 64:256], scale=0.125, bias=1024.4375)
        mask()
    wait("p", k_wt, kl8, kb2, k7, koff0, k_zr)
    mm(F[:, 0:64], I, T.zr[:], True, False)
    for i in range(3):
        gather(0, i)
    for t in range(1, 8):
        for i in range(4):
            offsets(t, i)
            gather(t - (i == 0), (i - 1) % 4)
    kf = gather(7, 3)
    kO = copyV(T.O[:], F[:, 0:64], kf)

    wait("g", kO)
    fused(lambda d: T.O[:, 8 * d:8 * d + 8], T.ri[me], "ar")
    wait("y", kO)
    Y.dma_start(out=T.ri[me], in_=T.O[:, 8 * me:8 * me + 8]).then_inc(sem.ar, 16)
    for e in (Y, S):
        e.wait_ge(sem.ar, both)
    Y.dma_start(out=T.last[:, :], in_=T.ri[:, 0:64, :]).then_inc(sem.fin, 16)
    S.dma_start(out=T.total[:, :], in_=T.ri[:, 64:128, :]).then_inc(sem.fin, 16)
    wait("g", ("v", cnt["v"]), ("s", cnt["s"]), ("p", cnt["p"]), ("gi", cnt["gi"]))
    g.wait_ge(sem.ls, 7 * (N - 1))
    g.wait_ge(sem.fin, 32)
